import numpy as np
import ml_dtypes


def mxq(x, axis, fmt="e4m3"):
    dtype, down = {"e4m3": (ml_dtypes.float8_e4m3fn, 7), "e5m2": (ml_dtypes.float8_e5m2, 14)}[fmt]
    v = np.moveaxis(np.asarray(x, np.float32).astype(ml_dtypes.bfloat16).astype(np.float64), axis, -1)
    blocks = v.reshape(v.shape[:-1] + (-1, 32))
    amax = np.abs(blocks).max(-1, keepdims=True)
    byte = np.maximum(np.where(amax > 0, np.frexp(amax)[1] - 1 + 127, 0) - down, 1)
    scale = np.exp2(byte - 127.0)
    codes = (blocks / scale).astype(np.float32).astype(dtype).astype(np.float64)
    return np.moveaxis((codes * scale).reshape(v.shape), -1, axis)


WIDE = False


def mx_kscale(k):
    if not WIDE:
        return np.ones(k)
    levels = np.array([10, -10, 5, -5, 0])
    if k % 512:
        return np.exp2(np.random.permutation(np.resize(levels, k // 32))).repeat(32)
    a = np.empty((k // 512, 16))
    for p in range(k // 512):
        a[p, :8] = np.random.permutation(np.resize(levels, 8))
        for g in range(8):
            far = levels[np.abs(levels - a[p, g]) >= 10]
            a[p, g + 8] = far[np.random.randint(len(far))]
    return np.exp2(a.ravel()).repeat(32)


BF16 = ml_dtypes.bfloat16


def bf(x):
    return np.asarray(x, np.float32).astype(BF16)


def f64(x):
    return np.asarray(x).astype(np.float64)


E2M1 = np.array([0.0, 0.5, 1.0, 1.5, 2.0, 3.0, 4.0, 6.0, -0.0, -0.5, -1.0, -1.5, -2.0, -3.0, -4.0, -6.0])


def pack_weight(w, fmt):
    k, n = w.shape
    w = f64(bf(w)).reshape(k // 32, 32, n)
    amax = np.abs(w).max(1)
    if fmt == "e4m3":
        byte = np.frexp(amax)[1] - 1 + 127 - 7
    else:
        mant, ex = np.frexp(amax / 6.0)
        byte = np.where(mant > 0.5, ex, ex - 1) + 127
    byte = np.clip(np.where(amax > 0, byte, 1), 1, 254)
    scaled = (w * np.exp2(127.0 - byte)[:, None, :]).reshape(k, n).astype(np.float32)
    by_word = np.ascontiguousarray(scaled.reshape(k // 512, 128, 4, n).transpose(0, 1, 3, 2))
    if fmt == "e4m3":
        words = by_word.astype(ml_dtypes.float8_e4m3fn).view(np.uint8)
    else:
        c = by_word.astype(ml_dtypes.float4_e2m1fn).view(np.uint8) & 0xF
        words = c[..., 0::2] | (c[..., 1::2] << 4)
    return np.ascontiguousarray(words), np.ascontiguousarray(byte.astype(np.uint8).reshape(k // 512, 16, n))


def unpack_weight(words, scales, fmt):
    g, p, n, _ = words.shape
    if fmt == "e4m3":
        vals = np.ascontiguousarray(words).view(ml_dtypes.float8_e4m3fn).astype(np.float64)
    else:
        nib = np.empty((g, p, n, 4), np.uint8)
        nib[..., 0::2] = words & 0xF
        nib[..., 1::2] = words >> 4
        vals = E2M1[nib]
    vals = vals * np.repeat(np.exp2(scales.astype(np.float64) - 127.0), 8, axis=1)[..., None]
    return vals.transpose(0, 1, 3, 2).reshape(g * 512, n)
def pack4(w):
    words, scales = pack_weight(w, "e2m1")
    return words.reshape(words.shape[0], 128, -1), scales


def unpack4(words, scales):
    return unpack_weight(words.reshape(words.shape[0], 128, -1, 2), scales, "e2m1")


M, C, H, G, D, S = 512, 2048, 4, 2, 512, 1024

EPS = 0.05
BASE = 10000.0
CAP = 5.0


def draw0():
    s, t = mx_kscale(C), mx_kscale(D)
    wq_words, wq_scales = pack4(np.random.standard_normal((C, H * D)) / np.sqrt(C) / s[:, None])
    position = np.random.randint(0, S, M)
    angle = position[:, None] * BASE ** (-np.arange(D // 2) / (D // 2))
    return {"x": bf(np.random.standard_normal((M, C)) * s),
            "wq_words": wq_words,
            "wq_scales": wq_scales,
            "gain": bf((1 + 0.1 * np.random.standard_normal(D)) * t),
            "cosines": bf(np.cos(angle)),
            "sines": bf(np.sin(angle)),
            "keys": bf(np.random.standard_normal((G, S, D)) / t)}


def rotate(z, c, s):
    even, odd = z[..., 0::2], z[..., 1::2]
    return np.stack([even * c - odd * s, even * s + odd * c], axis=-1).reshape(z.shape)


def core(x, wq_words, wq_scales, gain, cosines, sines, keys):
    y = mxq(f64(x), 1, "e4m3") @ unpack4(wq_words, wq_scales)
    y = y.reshape(M, H, D)
    a = y / np.sqrt(np.mean(y * y, axis=2, keepdims=True) + EPS) * f64(gain)
    b = rotate(a, f64(cosines)[:, None, :], f64(sines)[:, None, :])
    b = b.transpose(1, 0, 2).reshape(G, H // G * M, D)
    z = mxq(b, 2, "e4m3") @ mxq(f64(keys), 2, "e4m3").swapaxes(1, 2)
    return CAP * np.tanh(z.reshape(H, M, S) / (np.sqrt(D) * CAP))


def e4m3fn_bytes(y):
    return np.clip(np.asarray(y, np.float64), -448.0, 448.0).astype(np.float32).astype(ml_dtypes.float8_e4m3fn).view(np.uint8)


def e4m3fn_values(b):
    return np.asarray(b, np.uint8).view(ml_dtypes.float8_e4m3fn).astype(np.float64)


def setup_inputs():
    d = draw0()
    x0 = np.asarray(d['x']).astype(np.float64)
    s = (np.max(np.abs(x0), axis=(0,), keepdims=True) / 448.0).astype(np.float32)
    out = {}
    for k, v in d.items():
        if k == 'x':
            out['x_bytes'] = e4m3fn_bytes(x0 / s.astype(np.float64))
            out['x_scale'] = s
        else:
            out[k] = v
    return out


def reference(x_bytes, x_scale, wq_words, wq_scales, gain, cosines, sines, keys):
    return core(e4m3fn_values(x_bytes) * x_scale.astype(np.float64), wq_words, wq_scales, gain, cosines, sines, keys)

@@ -1,0 +1,396 @@
+import math
+from contextlib import ExitStack
+
+import concourse.mybir as mybir
+from concourse.masks import make_identity
+
+TOKENS, CHANNELS, HEADS, KEY_HEADS, FEATURES, KEYS = 512, 2048, 4, 2, 512, 1024
+EPS = 0.05
+CAP = 5.0
+
+FLOPS = 2 * TOKENS * CHANNELS * HEADS * FEATURES + 2 * HEADS * TOKENS * KEYS * FEATURES
+
+F32 = mybir.dt.float32
+BF16 = mybir.dt.bfloat16
+I32 = mybir.dt.int32
+U32 = mybir.dt.uint32
+U8 = mybir.dt.uint8
+FP8 = mybir.dt.float8_e4m3fn
+FP8X4 = mybir.dt.float8_e4m3fn_x4
+FP4X4 = mybir.dt.float4_e2m1fn_x4
+MULT = mybir.AluOpType.mult
+ADD = mybir.AluOpType.add
+POW = mybir.AluOpType.pow
+ACT = mybir.ActivationFunctionType
+
+P = 128
+PASSES = CHANNELS // 512
+M_TILES = TOKENS // P
+UNITS = M_TILES * HEADS
+HALF = KEYS // 2
+PAIRS = FEATURES // 2
+
+
+def tile_grouped_query_key_scores_f1_kernel(
+    tc, x_bytes, x_scale, wq_words, wq_scales, gain, cosines, sines, keys, out
+):
+    nc = tc.nc
+    with ExitStack() as ctx:
+        const = ctx.enter_context(tc.tile_pool(name="const", bufs=1))
+        work = ctx.enter_context(tc.tile_pool(name="work", bufs=3))
+        psum_y = ctx.enter_context(tc.psum_pool(name="psum_y", bufs=3))
+        psum_z = ctx.enter_context(tc.psum_pool(name="psum_z", bufs=3))
+        psum_t = ctx.enter_context(tc.psum_pool(name="psum_t", bufs=1))
+        ctx.enter_context(tc.manual_schedule())
+
+        ident = const.tile([P, P], F32, name="ident")
+        minus_half = const.tile([P, 1], F32, name="minus_half")
+        warm = const.tile([P, 1], F32, name="warm")
+        x_raw = [const.tile([P, CHANNELS], U8, name=f"x_raw{m}") for m in range(M_TILES)]
+        x_factor = const.tile([P, PASSES, 4], F32, name="x_factor")
+        w_codes = [const.tile([P, PASSES, 1024], U8, name=f"w_codes{h}", align_bytes=64) for h in range(HEADS)]
+        w_scales = const.tile([P, PASSES, HEADS * FEATURES], U8, name="w_scales", align_bytes=64)
+        k_raw = [const.tile([P, 8, FEATURES], BF16, name=f"k_raw{g}") for g in range(KEY_HEADS)]
+        k_codes = [const.tile([P, KEYS], U32, name=f"k_codes{g}", align_bytes=64) for g in range(KEY_HEADS)]
+        k_scales = [const.tile([P, KEYS], U8, name=f"k_scales{g}", align_bytes=64) for g in range(KEY_HEADS)]
+        trig = const.tile([P, M_TILES, 3, PAIRS], BF16, name="trig")
+        gain_all = const.tile([P, FEATURES], BF16, name="gain_all")
+        gain_odd = const.tile([P, PAIRS, 2], BF16, name="gain_odd")
+        table_even = [const.tile([P, FEATURES], F32, name=f"table_even{m}") for m in range(M_TILES)]
+        table_odd = [const.tile([P, FEATURES], F32, name=f"table_odd{m}") for m in range(M_TILES)]
+        x_codes = [const.tile([P, PASSES, P], U32, name=f"x_codes{m}", align_bytes=64) for m in range(M_TILES)]
+        x_scales = [const.tile([P, PASSES, P], U8, name=f"x_scales{m}", align_bytes=64) for m in range(M_TILES)]
+        x_bf = [const.tile([P, CHANNELS], BF16, name=f"x_bf{m}") for m in range(M_TILES)]
+        x_grouped = [const.tile([P, PASSES, P, 4], BF16, name=f"x_grouped{m}", align_bytes=64) for m in range(M_TILES)]
+        k_grouped = [
+            [const.tile([P, HALF, 4], BF16, name=f"k_grouped{g}{j}", align_bytes=64) for j in range(2)]
+            for g in range(KEY_HEADS)
+        ]
+
+        def load_x(m):
+            nc.sync.dma_start(out=x_raw[m][:], in_=x_bytes[m * P : (m + 1) * P, :])
+
+        def load_w(h):
+            nc.sync.dma_start(
+                out=w_codes[h][:], in_=wq_words[:, :, 1024 * h : 1024 * (h + 1)].rearrange("g p b -> p g b")
+            )
+
+        def load_keys(g, j):
+            nc.sync.dma_start(
+                out=k_raw[g][:, 4 * j : 4 * j + 4, :],
+                in_=keys[g, HALF * j : HALF * (j + 1), :].rearrange("(n p) d -> p n d", p=P),
+            )
+
+        nc.vector.memset(w_scales[:].rearrange("p g n -> p (g n)").bitcast(I32), 0)
+        nc.vector.memset(warm[:], 0.0)
+        load_x(0)
+        nc.scalar.dma_start(out=x_factor[:], in_=x_scale.rearrange("o (g p t) -> p (o g) t", p=P, t=4))
+        nc.scalar.dma_start(out=gain_all[:], in_=gain.partition_broadcast(P))
+        for j, source in enumerate((cosines, sines, cosines)):
+            nc.scalar.dma_start(out=trig[:, 0, j, :], in_=source[0:P, :])
+        nc.scalar.activation(out=warm[:], in_=warm[:], func=ACT.Tanh)
+        load_keys(0, 0)
+        w_scales_i32 = w_scales[:].rearrange("p g n -> p (g n)").bitcast(I32).rearrange("p (g n) -> p g n", g=PASSES)
+        wq_scales_i32 = wq_scales.bitcast(I32)
+        for q in range(4):
+            nc.sync.dma_start(
+                out=w_scales_i32[32 * q : 32 * q + 4],
+                in_=wq_scales_i32[:, 4 * q : 4 * q + 4, :].rearrange("g q n -> q g n"),
+            )
+        load_w(0)
+        load_keys(0, 1)
+        load_w(1)
+        load_x(1)
+        load_w(2)
+        load_keys(1, 0)
+        load_keys(1, 1)
+        load_w(3)
+        load_x(2)
+        load_x(3)
+        for j, source in enumerate((cosines, sines, cosines)):
+            nc.sync.dma_start(
+                out=trig[:, 1:M_TILES, j, :], in_=source[P:TOKENS, :].rearrange("(m p) i -> p m i", p=P)
+            )
+
+        make_identity(nc, ident[:])
+        nc.gpsimd.memset(minus_half[:], -0.5)
+        for e, sign in ((0, -1.0), (1, 1.0)):
+            nc.gpsimd.tensor_scalar(
+                out=gain_odd[:, :, e], in0=gain_all[:, 1:FEATURES:2], scalar1=sign, scalar2=0.0, op0=MULT, op1=ADD
+            )
+
+        def make_table(m, odd):
+            table, factors = (
+                (table_odd[m], gain_odd[:])
+                if odd
+                else (table_even[m], gain_all[:, 0:FEATURES:2].unsqueeze(2).to_broadcast([P, PAIRS, 2]))
+            )
+            nc.gpsimd.tensor_tensor(
+                out=table[:].rearrange("p (i e) -> p i e", e=2),
+                in0=trig[:, m, odd : odd + 2, :].rearrange("p e i -> p i e"),
+                in1=factors,
+                op=MULT,
+            )
+
+        def widen_x(engine, m, g):
+            cols = slice(512 * g, 512 * (g + 1))
+            src = x_raw[m][:, cols].bitcast(FP8)
+            if engine == "vector":
+                nc.vector.tensor_copy(out=x_bf[m][:, cols], in_=src)
+            else:
+                nc.scalar.copy(out=x_bf[m][:, cols], in_=src)
+
+        def transpose_x(m, g, pool, tag):
+            bank = pool.tile([P, 512], F32, name=tag)
+            words = x_bf[m][:].bitcast(F32)
+            for u in range(2):
+                nc.tensor.transpose(
+                    bank[:, P * u : P * (u + 1)], words[:, 256 * g + u : 256 * (g + 1) : 2], ident[:]
+                )
+            return bank
+
+        def scale_x(m, g, bank):
+            nc.vector.tensor_tensor(
+                out=x_grouped[m][:, g].rearrange("p r (u e) -> p r u e", u=2),
+                in0=bank[:, 0 : 2 * P].bitcast(BF16).rearrange("p (u r e) -> p r u e", u=2, e=2),
+                in1=x_factor[:, g, :]
+                .rearrange("p (u e) -> p u e", u=2)
+                .unsqueeze(1)
+                .to_broadcast([P, P, 2, 2]),
+                op=MULT,
+            )
+
+        def quantize_x(m, g0, g1):
+            nc.vector.quantize_mx(
+                out=x_codes[m][:, g0:g1].rearrange("p g r -> p (g r)").bitcast(FP8X4),
+                scales=x_scales[m][:, g0:g1].rearrange("p g r -> p (g r)"),
+                in_=x_grouped[m][:, g0:g1].rearrange("p g r t -> p (g r t)"),
+            )
+
+        def transpose_keys(g, i, pool, tag):
+            bank = pool.tile([P, 512], F32, name=tag)
+            for n in range(2):
+                words = k_raw[g][:, 2 * i + n, :].bitcast(F32)
+                for u in range(2):
+                    c = (2 * n + u) * P
+                    nc.tensor.transpose(bank[:, c : c + P], words[:, u:256:2], ident[:])
+            return bank
+
+        def group_keys(g, i, bank):
+            c = 256 * (i % 2)
+            nc.scalar.copy(
+                out=k_grouped[g][i // 2][:, c : c + 256, :]
+                .rearrange("p r t -> p (r t)")
+                .bitcast(F32)
+                .rearrange("p (n r u) -> p n r u", n=2, u=2),
+                in_=bank[:].rearrange("p (n u r) -> p n r u", n=2, u=2),
+            )
+
+        def quantize_keys(g, j):
+            cols = slice(HALF * j, HALF * (j + 1))
+            nc.vector.quantize_mx(
+                out=k_codes[g][:, cols].bitcast(FP8X4),
+                scales=k_scales[g][:, cols],
+                in_=k_grouped[g][j][:].rearrange("p r t -> p (r t)"),
+            )
+
+        y_banks, r_tiles, p_tiles, b_tiles, bt_tiles, bq_tiles, z_banks, tanh_tiles = {}, {}, {}, {}, {}, {}, {}, {}
+
+        def project(s):
+            m, h = divmod(s, HEADS)
+            y = psum_y.tile([P, 512], F32, name="y")
+            for g in range(PASSES):
+                nc.tensor.matmul_mx(
+                    out=y[:],
+                    lhsT=x_codes[m][:, g, :].bitcast(FP8X4),
+                    lhsT_scale=x_scales[m][:, g, :],
+                    rhs=w_codes[h][:, g, :].bitcast(FP4X4),
+                    rhs_scale=w_scales[:, g, FEATURES * h : FEATURES * (h + 1)],
+                    start=(g == 0),
+                    stop=(g == PASSES - 1),
+                )
+            y_banks[s] = y
+
+        def square(s):
+            junk = work.tile([P, FEATURES], BF16, name="junk")
+            total = work.tile([P, 1], F32, name="total")
+            nc.scalar.activation(out=junk[:], in_=y_banks[s][:], func=ACT.Square, accum_out=total[:])
+            r_tiles[s] = total
+
+        def inverse_rms(s):
+            mean = work.tile([P, 1], F32, name="mean")
+            inv = work.tile([P, 1], F32, name="inv")
+            nc.gpsimd.tensor_scalar(
+                out=mean[:], in0=r_tiles[s][:], scalar1=1.0 / FEATURES, scalar2=EPS, op0=MULT, op1=ADD
+            )
+            nc.gpsimd.tensor_tensor(out=inv[:], in0=mean[:], in1=minus_half[:], op=POW)
+            r_tiles[s] = inv
+
+        def rotate_part(s, odd):
+            m = s // HEADS
+            part = work.tile([P, FEATURES], F32, name="part_odd" if odd else "part_even")
+            table = table_odd[m] if odd else table_even[m]
+            nc.vector.scalar_tensor_tensor(
+                out=part[:].rearrange("p (i e) -> p i e", e=2),
+                in0=y_banks[s][:, odd:FEATURES:2].unsqueeze(2).to_broadcast([P, PAIRS, 2]),
+                scalar=r_tiles[s][:],
+                in1=table[:].rearrange("p (i e) -> p i e", e=2),
+                op0=MULT,
+                op1=MULT,
+            )
+            p_tiles[s, odd] = part
+
+        def rotate_add(s):
+            b = work.tile([P, FEATURES], BF16, name="b")
+            nc.vector.tensor_tensor(
+                out=b[:].rearrange("p (u k e) -> p u k e", u=2, e=2),
+                in0=p_tiles[s, 0][:].rearrange("p (k u e) -> p u k e", u=2, e=2),
+                in1=p_tiles[s, 1][:].rearrange("p (k u e) -> p u k e", u=2, e=2),
+                op=ADD,
+            )
+            b_tiles[s] = b
+
+        def transpose_b(s):
+            bank = psum_t.tile([P, 512], F32, name="tb")
+            words = b_tiles[s][:].bitcast(F32)
+            for u in range(2):
+                nc.tensor.transpose(bank[:, P * u : P * (u + 1)], words[:, P * u : P * (u + 1)], ident[:])
+            bt_tiles[s] = bank
+
+        def group_b(s):
+            grouped = work.tile([P, P, 4], BF16, name="b_grouped", align_bytes=64)
+            nc.scalar.copy(
+                out=grouped[:].rearrange("p r t -> p (r t)").bitcast(F32).rearrange("p (r u) -> p r u", u=2),
+                in_=bt_tiles[s][:, 0 : 2 * P].rearrange("p (u r) -> p r u", u=2),
+            )
+            bt_tiles[s] = grouped
+
+        def quantize_b(s):
+            codes = work.tile([P, P], U32, name="b_codes", align_bytes=64)
+            scales = work.tile([P, P], U8, name="b_scales", align_bytes=64)
+            nc.vector.quantize_mx(
+                out=codes[:].bitcast(FP8X4), scales=scales[:], in_=bt_tiles[s][:].rearrange("p r t -> p (r t)")
+            )
+            bq_tiles[s] = (codes, scales)
+
+        def score(s, j):
+            g = (s % HEADS) // (HEADS // KEY_HEADS)
+            codes, scales = bq_tiles[s]
+            cols = slice(HALF * j, HALF * (j + 1))
+            z = psum_z.tile([P, 512], F32, name="z")
+            nc.tensor.matmul_mx(
+                out=z[:],
+                lhsT=codes[:].bitcast(FP8X4),
+                lhsT_scale=scales[:],
+                rhs=k_codes[g][:, cols].bitcast(FP8X4),
+                rhs_scale=k_scales[g][:, cols],
+                start=True,
+                stop=True,
+            )
+            z_banks[s, j] = z
+
+        def cap_tanh(s, j):
+            if j == 0:
+                tanh_tile = work.tile([P, KEYS], F32, name="tanh_tile")
+                tanh_tiles[s] = tanh_tile
+            nc.scalar.activation(
+                out=tanh_tiles[s][:, HALF * j : HALF * (j + 1)],
+                in_=z_banks[s, j][:],
+                func=ACT.Tanh,
+                scale=1.0 / (CAP * math.sqrt(FEATURES)),
+            )
+
+        def finish(s):
+            m, h = divmod(s, HEADS)
+            result = work.tile([P, KEYS], F32, name="result")
+            rows = slice(m * P, (m + 1) * P)
+            if s < UNITS - 2:
+                nc.gpsimd.tensor_scalar(
+                    out=result[:], in0=tanh_tiles[s][:], scalar1=CAP, scalar2=0.0, op0=MULT, op1=ADD
+                )
+                nc.sync.dma_start(out=out[h, rows, :], in_=result[:])
+            else:
+                for j in range(2):
+                    cols = slice(HALF * j, HALF * (j + 1))
+                    nc.vector.tensor_scalar(
+                        out=result[:, cols], in0=tanh_tiles[s][:, cols], scalar1=CAP, scalar2=None, op0=MULT
+                    )
+                    nc.sync.dma_start(out=out[h, rows, cols], in_=result[:, cols])
+
+        for g in range(2):
+            widen_x("vector", 0, g)
+        for g in range(2, 4):
+            widen_x("scalar", 0, g)
+        make_table(0, 0)
+        make_table(0, 1)
+        x_banks = [transpose_x(0, g, psum_z if g < 3 else psum_t, "z" if g < 3 else "tx") for g in range(PASSES)]
+        for g in range(PASSES):
+            scale_x(0, g, x_banks[g])
+            if g % 2 == 1 and g > 1:
+                quantize_x(0, 0, 2)
+        quantize_x(0, 2, 4)
+        k_banks = [transpose_keys(0, i, psum_y, "y") for i in range(3)]
+        for i in range(3):
+            group_keys(0, i, k_banks[i])
+        last = transpose_keys(0, 3, psum_z, "z")
+        group_keys(0, 3, last)
+        quantize_keys(0, 0)
+        quantize_keys(0, 1)
+        project(0)
+        project(1)
+        square(0)
+        square(1)
+        inverse_rms(0)
+        inverse_rms(1)
+
+        pieces = {}
+        for m in range(1, M_TILES):
+            for g in range(PASSES):
+                pieces.setdefault(max(4 * m - 6 + g, g // 2), []).append((m, g))
+        for m, g in pieces[0]:
+            widen_x("scalar", m, g)
+
+        for s in range(UNITS + 2):
+            if 0 <= s - 1 < UNITS:
+                transpose_b(s - 1)
+            now = pieces.get(s, [])
+            x_banks = [transpose_x(m, g, psum_t, "tx") for m, g in now[:1]]
+            if 0 <= s - 2 < UNITS:
+                cap_tanh(s - 2, 0)
+            if 0 <= s - 1 < UNITS:
+                group_b(s - 1)
+            if 0 <= s - 2 < UNITS:
+                cap_tanh(s - 2, 1)
+            if s < UNITS:
+                rotate_part(s, 0)
+                rotate_part(s, 1)
+            for bank, (m, g) in zip(x_banks, now):
+                scale_x(m, g, bank)
+            for m, g in now[1:]:
+                scale_x(m, g, transpose_x(m, g, psum_t, "tx"))
+            if 0 <= s - 1 < UNITS:
+                quantize_b(s - 1)
+            if s < UNITS:
+                rotate_add(s)
+            for m, g in now:
+                if g == PASSES - 1:
+                    quantize_x(m, 0, PASSES)
+            if s < 2:
+                for i in (2 * s, 2 * s + 1):
+                    group_keys(1, i, transpose_keys(1, i, psum_z, "z"))
+                quantize_keys(1, s)
+            if s + 2 < UNITS:
+                project(s + 2)
+            if 0 <= s - 1 < UNITS:
+                score(s - 1, 0)
+                score(s - 1, 1)
+            if s + 2 < UNITS:
+                square(s + 2)
+            for m, g in pieces.get(s + 1, []):
+                widen_x("scalar", m, g)
+            if 0 <= s - 2 < UNITS:
+                finish(s - 2)
+            if s + 2 < UNITS:
+                inverse_rms(s + 2)
+            if s % 4 < 2 and s // 4 + 1 < M_TILES:
+                make_table(s // 4 + 1, s % 4)

@@ -29,6 +29,7 @@ M_TILES = TOKENS // P
 UNITS = M_TILES * HEADS
 HALF = KEYS // 2
 PAIRS = FEATURES // 2
+FINISH = ("v", "s")
 
 
 def tile_grouped_query_key_scores_f1_kernel(
@@ -89,7 +90,7 @@ def tile_grouped_query_key_scores_f1_kernel(
         for j, source in enumerate((cosines, sines, cosines)):
             nc.scalar.dma_start(out=trig[:, 0, j, :], in_=source[0:P, :])
         nc.scalar.activation(out=warm[:], in_=warm[:], func=ACT.Tanh)
-        load_keys(0, 0)
+        load_x(1)
         w_scales_i32 = w_scales[:].rearrange("p g n -> p (g n)").bitcast(I32).rearrange("p (g n) -> p g n", g=PASSES)
         wq_scales_i32 = wq_scales.bitcast(I32)
         for q in range(4):
@@ -98,19 +99,19 @@ def tile_grouped_query_key_scores_f1_kernel(
                 in_=wq_scales_i32[:, 4 * q : 4 * q + 4, :].rearrange("g q n -> q g n"),
             )
         load_w(0)
+        load_keys(0, 0)
         load_keys(0, 1)
         load_w(1)
-        load_x(1)
         load_w(2)
         load_keys(1, 0)
         load_keys(1, 1)
         load_w(3)
-        load_x(2)
-        load_x(3)
         for j, source in enumerate((cosines, sines, cosines)):
             nc.sync.dma_start(
                 out=trig[:, 1:M_TILES, j, :], in_=source[P:TOKENS, :].rearrange("(m p) i -> p m i", p=P)
             )
+        load_x(2)
+        load_x(3)
 
         make_identity(nc, ident[:])
         nc.gpsimd.memset(minus_half[:], -0.5)
@@ -194,7 +195,7 @@ def tile_grouped_query_key_scores_f1_kernel(
                 in_=k_grouped[g][j][:].rearrange("p r t -> p (r t)"),
             )
 
-        y_banks, r_tiles, p_tiles, b_tiles, bt_tiles, bq_tiles, z_banks, tanh_tiles = {}, {}, {}, {}, {}, {}, {}, {}
+        y_banks, r_tiles, p_tiles, b_tiles, bt_tiles, bq_tiles, z_banks, tanh_tiles, results = {}, {}, {}, {}, {}, {}, {}, {}, {}
 
         def project(s):
             m, h = divmod(s, HEADS)
@@ -300,61 +301,81 @@ def tile_grouped_query_key_scores_f1_kernel(
                 scale=1.0 / (CAP * math.sqrt(FEATURES)),
             )
 
-        def finish(s):
+        def finish(s, j):
             m, h = divmod(s, HEADS)
-            result = work.tile([P, KEYS], F32, name="result")
+            if j == 0:
+                result = work.tile([P, KEYS], F32, name="result")
+                results[s] = result
             rows = slice(m * P, (m + 1) * P)
-            if s < UNITS - 2:
-                nc.gpsimd.tensor_scalar(
-                    out=result[:], in0=tanh_tiles[s][:], scalar1=CAP, scalar2=0.0, op0=MULT, op1=ADD
-                )
-                nc.sync.dma_start(out=out[h, rows, :], in_=result[:])
+            cols = slice(HALF * j, HALF * (j + 1))
+            src, dst = tanh_tiles[s][:, cols], results[s][:, cols]
+            who = FINISH[j]
+            if s >= UNITS - 1:
+                who = "v"
+            if who == "v":
+                nc.vector.tensor_scalar(out=dst, in0=src, scalar1=CAP, scalar2=None, op0=MULT)
+            elif who == "g":
+                nc.gpsimd.tensor_scalar(out=dst, in0=src, scalar1=CAP, scalar2=0.0, op0=MULT, op1=ADD)
             else:
-                for j in range(2):
-                    cols = slice(HALF * j, HALF * (j + 1))
-                    nc.vector.tensor_scalar(
-                        out=result[:, cols], in0=tanh_tiles[s][:, cols], scalar1=CAP, scalar2=None, op0=MULT
-                    )
-                    nc.sync.dma_start(out=out[h, rows, cols], in_=result[:, cols])
+                nc.scalar.activation(out=dst, in_=src, func=ACT.Copy, scale=CAP)
+            if s >= UNITS - 1:
+                nc.sync.dma_start(out=out[h, rows, cols], in_=dst)
+            elif j == 1:
+                nc.sync.dma_start(out=out[h, rows, :], in_=results[s][:])
 
-        for g in range(2):
-            widen_x("vector", 0, g)
-        for g in range(2, 4):
-            widen_x("scalar", 0, g)
+        widen_x("vector", 0, 0)
+        widen_x("scalar", 0, 2)
+        widen_x("vector", 0, 1)
+        widen_x("scalar", 0, 3)
         make_table(0, 0)
         make_table(0, 1)
-        x_banks = [transpose_x(0, g, psum_z if g < 3 else psum_t, "z" if g < 3 else "tx") for g in range(PASSES)]
+        x_banks = [
+            transpose_x(0, 0, psum_z, "z"),
+            transpose_x(0, 1, psum_z, "z"),
+            transpose_x(0, 2, psum_z, "z"),
+            transpose_x(0, 3, psum_t, "tx"),
+        ]
         for g in range(PASSES):
-            scale_x(0, g, x_banks[g])
-            if g % 2 == 1 and g > 1:
-                quantize_x(0, 0, 2)
-        quantize_x(0, 2, 4)
-        k_banks = [transpose_keys(0, i, psum_y, "y") for i in range(3)]
-        for i in range(3):
-            group_keys(0, i, k_banks[i])
-        last = transpose_keys(0, 3, psum_z, "z")
-        group_keys(0, 3, last)
-        quantize_keys(0, 0)
-        quantize_keys(0, 1)
+            widen_x("scalar", 1, g)
+        scale_x(0, 0, x_banks[0])
+        scale_x(0, 1, x_banks[1])
+        quantize_x(0, 0, 1)
+        scale_x(0, 2, x_banks[2])
+        quantize_x(0, 1, 2)
+        scale_x(0, 3, x_banks[3])
+        quantize_x(0, 2, 3)
+        y_first = transpose_x(1, 0, psum_t, "tb")
+        y_second = transpose_x(1, 1, psum_y, "y")
+        k_banks = [transpose_keys(0, 0, psum_z, "z"), transpose_keys(0, 1, psum_z, "z")]
+        group_keys(0, 0, k_banks[0])
+        group_keys(0, 1, k_banks[1])
+        scale_x(1, 0, y_first)
+        quantize_x(0, 3, 4)
         project(0)
-        project(1)
+        x_banks = [transpose_x(1, 2, psum_t, "tx"), transpose_x(1, 3, psum_y, "y")]
+        scale_x(1, 1, y_second)
         square(0)
-        square(1)
+        k_banks = [transpose_keys(0, 2, psum_z, "z"), transpose_keys(0, 3, psum_z, "z")]
+        group_keys(0, 2, k_banks[0])
+        scale_x(1, 2, x_banks[0])
+        scale_x(1, 3, x_banks[1])
         inverse_rms(0)
+        project(1)
+        square(1)
         inverse_rms(1)
+        group_keys(0, 3, k_banks[1])
 
         pieces = {}
-        for m in range(1, M_TILES):
+        for m in range(2, M_TILES):
             for g in range(PASSES):
-                pieces.setdefault(max(4 * m - 6 + g, g // 2), []).append((m, g))
-        for m, g in pieces[0]:
-            widen_x("scalar", m, g)
+                pieces.setdefault(4 * m - 6 + g, []).append((m, g))
+        quants = {0: ((0, 0), (0, 1)), 1: ((1, 0),), 2: ((1, 1),)}
 
         for s in range(UNITS + 2):
             if 0 <= s - 1 < UNITS:
                 transpose_b(s - 1)
             now = pieces.get(s, [])
-            x_banks = [transpose_x(m, g, psum_t, "tx") for m, g in now[:1]]
+            x_banks = [transpose_x(m, g, psum_t, "tx") for m, g in now]
             if 0 <= s - 2 < UNITS:
                 cap_tanh(s - 2, 0)
             if 0 <= s - 1 < UNITS:
@@ -364,21 +385,25 @@ def tile_grouped_query_key_scores_f1_kernel(
             if s < UNITS:
                 rotate_part(s, 0)
                 rotate_part(s, 1)
+            if s == 0:
+                quantize_x(1, 0, PASSES)
             for bank, (m, g) in zip(x_banks, now):
                 scale_x(m, g, bank)
-            for m, g in now[1:]:
-                scale_x(m, g, transpose_x(m, g, psum_t, "tx"))
+            for g, j in quants.get(s, ()):
+                quantize_keys(g, j)
             if 0 <= s - 1 < UNITS:
                 quantize_b(s - 1)
             if s < UNITS:
                 rotate_add(s)
+            if 0 <= s - 2 < UNITS:
+                finish(s - 2, 0)
+                finish(s - 2, 1)
             for m, g in now:
                 if g == PASSES - 1:
                     quantize_x(m, 0, PASSES)
             if s < 2:
                 for i in (2 * s, 2 * s + 1):
                     group_keys(1, i, transpose_keys(1, i, psum_z, "z"))
-                quantize_keys(1, s)
             if s + 2 < UNITS:
                 project(s + 2)
             if 0 <= s - 1 < UNITS:
@@ -388,9 +413,7 @@ def tile_grouped_query_key_scores_f1_kernel(
                 square(s + 2)
             for m, g in pieces.get(s + 1, []):
                 widen_x("scalar", m, g)
-            if 0 <= s - 2 < UNITS:
-                finish(s - 2)
             if s + 2 < UNITS:
                 inverse_rms(s + 2)
-            if s % 4 < 2 and s // 4 + 1 < M_TILES:
-                make_table(s // 4 + 1, s % 4)
+            if s // 2 + 1 < M_TILES:
+                make_table(s // 2 + 1, s % 2)

@@ -20,7 +20,6 @@ FP8X4 = mybir.dt.float8_e4m3fn_x4
 FP4X4 = mybir.dt.float4_e2m1fn_x4
 MULT = mybir.AluOpType.mult
 ADD = mybir.AluOpType.add
-POW = mybir.AluOpType.pow
 ACT = mybir.ActivationFunctionType
 
 P = 128
@@ -29,7 +28,15 @@ M_TILES = TOKENS // P
 UNITS = M_TILES * HEADS
 HALF = KEYS // 2
 PAIRS = FEATURES // 2
-FINISH = ("v", "s")
+SEED_BITS = 0x5F3759DF - (1 << 22) - (1 << 30)
+
+
+def finisher(s, j):
+    if s >= 14:
+        return "v"
+    if s < 2:
+        return "vs"[j]
+    return "g" if j == 0 else "vs"[s % 2]
 
 
 def tile_grouped_query_key_scores_f1_kernel(
@@ -39,15 +46,15 @@ def tile_grouped_query_key_scores_f1_kernel(
     with ExitStack() as ctx:
         const = ctx.enter_context(tc.tile_pool(name="const", bufs=1))
         work = ctx.enter_context(tc.tile_pool(name="work", bufs=3))
-        psum_y = ctx.enter_context(tc.psum_pool(name="psum_y", bufs=3))
-        psum_z = ctx.enter_context(tc.psum_pool(name="psum_z", bufs=3))
+        psum_y = ctx.enter_context(tc.psum_pool(name="psum_y", bufs=4))
+        psum_z = ctx.enter_context(tc.psum_pool(name="psum_z", bufs=2))
         psum_t = ctx.enter_context(tc.psum_pool(name="psum_t", bufs=1))
         ctx.enter_context(tc.manual_schedule())
 
         ident = const.tile([P, P], F32, name="ident")
-        minus_half = const.tile([P, 1], F32, name="minus_half")
         warm = const.tile([P, 1], F32, name="warm")
         x_raw = [const.tile([P, CHANNELS], U8, name=f"x_raw{m}") for m in range(M_TILES)]
+        x_wide = const.tile([P, CHANNELS], F32, name="x_wide")
         x_factor = const.tile([P, PASSES, 4], F32, name="x_factor")
         w_codes = [const.tile([P, PASSES, 1024], U8, name=f"w_codes{h}", align_bytes=64) for h in range(HEADS)]
         w_scales = const.tile([P, PASSES, HEADS * FEATURES], U8, name="w_scales", align_bytes=64)
@@ -55,8 +62,10 @@ def tile_grouped_query_key_scores_f1_kernel(
         k_codes = [const.tile([P, KEYS], U32, name=f"k_codes{g}", align_bytes=64) for g in range(KEY_HEADS)]
         k_scales = [const.tile([P, KEYS], U8, name=f"k_scales{g}", align_bytes=64) for g in range(KEY_HEADS)]
         trig = const.tile([P, M_TILES, 3, PAIRS], BF16, name="trig")
-        gain_all = const.tile([P, FEATURES], BF16, name="gain_all")
-        gain_odd = const.tile([P, PAIRS, 2], BF16, name="gain_odd")
+        gain_row = const.tile([P, FEATURES], BF16, name="gain_row")
+        ones = const.tile([P, P], BF16, name="ones")
+        gain_all = const.tile([P, FEATURES], F32, name="gain_all")
+        gain_odd = const.tile([P, PAIRS, 2], F32, name="gain_odd")
         table_even = [const.tile([P, FEATURES], F32, name=f"table_even{m}") for m in range(M_TILES)]
         table_odd = [const.tile([P, FEATURES], F32, name=f"table_odd{m}") for m in range(M_TILES)]
         x_codes = [const.tile([P, PASSES, P], U32, name=f"x_codes{m}", align_bytes=64) for m in range(M_TILES)]
@@ -78,15 +87,18 @@ def tile_grouped_query_key_scores_f1_kernel(
 
         def load_keys(g, j):
             nc.sync.dma_start(
-                out=k_raw[g][:, 4 * j : 4 * j + 4, :],
-                in_=keys[g, HALF * j : HALF * (j + 1), :].rearrange("(n p) d -> p n d", p=P),
+                out=k_raw[g][:, 4 * j : 4 * j + 4, :].rearrange("p (n i) d -> p n (i d)", i=2),
+                in_=keys[g, HALF * j : HALF * (j + 1), :].rearrange("(n p i) d -> p n (i d)", p=P, i=2),
             )
 
-        nc.vector.memset(w_scales[:].rearrange("p g n -> p (g n)").bitcast(I32), 0)
+        make_identity(nc, ident[:])
         nc.vector.memset(warm[:], 0.0)
+        nc.vector.memset(gain_row[:], 0.0)
+        nc.vector.memset(ones[:], 1.0)
+        nc.vector.memset(w_scales[:].rearrange("p g n -> p (g n)").bitcast(I32), 0)
         load_x(0)
         nc.scalar.dma_start(out=x_factor[:], in_=x_scale.rearrange("o (g p t) -> p (o g) t", p=P, t=4))
-        nc.scalar.dma_start(out=gain_all[:], in_=gain.partition_broadcast(P))
+        nc.scalar.dma_start(out=gain_row[0:1, :], in_=gain.unsqueeze(0))
         for j, source in enumerate((cosines, sines, cosines)):
             nc.scalar.dma_start(out=trig[:, 0, j, :], in_=source[0:P, :])
         nc.scalar.activation(out=warm[:], in_=warm[:], func=ACT.Tanh)
@@ -100,35 +112,31 @@ def tile_grouped_query_key_scores_f1_kernel(
             )
         load_w(0)
         load_keys(0, 0)
-        load_keys(0, 1)
         load_w(1)
-        load_w(2)
-        load_keys(1, 0)
-        load_keys(1, 1)
-        load_w(3)
         for j, source in enumerate((cosines, sines, cosines)):
             nc.sync.dma_start(
                 out=trig[:, 1:M_TILES, j, :], in_=source[P:TOKENS, :].rearrange("(m p) i -> p m i", p=P)
             )
+        load_w(2)
+        load_keys(0, 1)
+        load_w(3)
+        load_keys(1, 0)
+        nc.sync.dma_start(out=x_wide[:], in_=x_scale.rearrange("o k -> (o k)").partition_broadcast(P))
         load_x(2)
+        load_keys(1, 1)
         load_x(3)
 
-        make_identity(nc, ident[:])
-        nc.gpsimd.memset(minus_half[:], -0.5)
-        for e, sign in ((0, -1.0), (1, 1.0)):
-            nc.gpsimd.tensor_scalar(
-                out=gain_odd[:, :, e], in0=gain_all[:, 1:FEATURES:2], scalar1=sign, scalar2=0.0, op0=MULT, op1=ADD
-            )
-
-        def make_table(m, odd):
-            table, factors = (
-                (table_odd[m], gain_odd[:])
-                if odd
-                else (table_even[m], gain_all[:, 0:FEATURES:2].unsqueeze(2).to_broadcast([P, PAIRS, 2]))
-            )
+        def make_table(m, odd, part=None):
+            pairs = slice(0, PAIRS) if part is None else slice(PAIRS // 2 * part, PAIRS // 2 * (part + 1))
+            n = pairs.stop - pairs.start
+            table = table_odd[m] if odd else table_even[m]
+            if odd:
+                factors = gain_odd[:, pairs, :]
+            else:
+                factors = gain_all[:, 2 * pairs.start : 2 * pairs.stop : 2].unsqueeze(2).to_broadcast([P, n, 2])
             nc.gpsimd.tensor_tensor(
-                out=table[:].rearrange("p (i e) -> p i e", e=2),
-                in0=trig[:, m, odd : odd + 2, :].rearrange("p e i -> p i e"),
+                out=table[:].rearrange("p (i e) -> p i e", e=2)[:, pairs, :],
+                in0=trig[:, m, odd : odd + 2, pairs].rearrange("p e i -> p i e"),
                 in1=factors,
                 op=MULT,
             )
@@ -168,6 +176,31 @@ def tile_grouped_query_key_scores_f1_kernel(
                 in_=x_grouped[m][:, g0:g1].rearrange("p g r t -> p (g r t)"),
             )
 
+        def multiply_x(m, half):
+            cols = slice(1024 * half, 1024 * (half + 1))
+            nc.vector.tensor_tensor(
+                out=x_bf[m][:, cols], in0=x_raw[m][:, cols].bitcast(FP8), in1=x_wide[:, cols], op=MULT
+            )
+
+        def turn_x(m, half):
+            bank = psum_t.tile([P, 512], F32, name="tx")
+            words = x_bf[m][:].bitcast(F32)
+            for g in (0, 1):
+                for u in (0, 1):
+                    first = 512 * half + 256 * g + u
+                    c = (2 * g + u) * P
+                    nc.tensor.transpose(bank[:, c : c + P], words[:, first : 512 * half + 256 * (g + 1) : 2], ident[:])
+            return bank
+
+        def group_x(m, half, bank):
+            nc.scalar.copy(
+                out=x_grouped[m][:, 2 * half : 2 * half + 2]
+                .rearrange("p g r t -> p (g r t)")
+                .bitcast(F32)
+                .rearrange("p (g r u) -> p g r u", g=2, u=2),
+                in_=bank[:].rearrange("p (g u r) -> p g r u", g=2, u=2),
+            )
+
         def transpose_keys(g, i, pool, tag):
             bank = pool.tile([P, 512], F32, name=tag)
             for n in range(2):
@@ -183,8 +216,8 @@ def tile_grouped_query_key_scores_f1_kernel(
                 out=k_grouped[g][i // 2][:, c : c + 256, :]
                 .rearrange("p r t -> p (r t)")
                 .bitcast(F32)
-                .rearrange("p (n r u) -> p n r u", n=2, u=2),
-                in_=bank[:].rearrange("p (n u r) -> p n r u", n=2, u=2),
+                .rearrange("p (r c) -> p r c", c=4),
+                in_=bank[:].rearrange("p (c r) -> p r c", c=4),
             )
 
         def quantize_keys(g, j):
@@ -195,7 +228,7 @@ def tile_grouped_query_key_scores_f1_kernel(
                 in_=k_grouped[g][j][:].rearrange("p r t -> p (r t)"),
             )
 
-        y_banks, r_tiles, p_tiles, b_tiles, bt_tiles, bq_tiles, z_banks, tanh_tiles, results = {}, {}, {}, {}, {}, {}, {}, {}, {}
+        results, change_tiles, half_tiles, y_banks, r_tiles, p_tiles, b_tiles, bt_tiles, bq_tiles, z_banks, tanh_tiles = {}, {}, {}, {}, {}, {}, {}, {}, {}, {}, {}
 
         def project(s):
             m, h = divmod(s, HEADS)
@@ -214,18 +247,48 @@ def tile_grouped_query_key_scores_f1_kernel(
 
         def square(s):
             junk = work.tile([P, FEATURES], BF16, name="junk")
-            total = work.tile([P, 1], F32, name="total")
+            total = work.tile([P, 1], F32, name="total", bufs=6)
             nc.scalar.activation(out=junk[:], in_=y_banks[s][:], func=ACT.Square, accum_out=total[:])
             r_tiles[s] = total
 
-        def inverse_rms(s):
-            mean = work.tile([P, 1], F32, name="mean")
-            inv = work.tile([P, 1], F32, name="inv")
-            nc.gpsimd.tensor_scalar(
-                out=mean[:], in0=r_tiles[s][:], scalar1=1.0 / FEATURES, scalar2=EPS, op0=MULT, op1=ADD
+        def half_mean(s):
+            half = work.tile([P, 1], F32, name="half", bufs=6)
+            nc.vector.tensor_scalar(
+                out=half[:], in0=r_tiles[s][:], scalar1=-0.5 / FEATURES, scalar2=-0.5 * EPS, op0=MULT, op1=ADD
             )
-            nc.gpsimd.tensor_tensor(out=inv[:], in0=mean[:], in1=minus_half[:], op=POW)
-            r_tiles[s] = inv
+            half_tiles[s] = half
+
+        def first_guess(s):
+            seed = work.tile([P, 1], I32, name="seed", bufs=6)
+            nc.vector.tensor_scalar(
+                out=seed[:],
+                in0=half_tiles[s][:].bitcast(I32),
+                scalar1=-0.5,
+                scalar2=float(SEED_BITS),
+                op0=MULT,
+                op1=ADD,
+            )
+            r_tiles[s] = seed[:].bitcast(F32)
+
+        def newton_a(s):
+            guess = r_tiles[s]
+            change = work.tile([P, 1], F32, name="change", bufs=6)
+            nc.gpsimd.tensor_scalar(
+                out=change[:], in0=guess, scalar1=guess, scalar2=half_tiles[s][:], op0=MULT, op1=MULT
+            )
+            change_tiles[s] = change
+
+        def newton_b(s):
+            better = work.tile([P, 1], F32, name="better", bufs=12)
+            nc.gpsimd.tensor_scalar(
+                out=better[:], in0=change_tiles[s][:], scalar1=1.5, scalar2=r_tiles[s], op0=ADD, op1=MULT
+            )
+            r_tiles[s] = better[:]
+
+        def newton(s, steps):
+            for i in range(steps):
+                newton_a(s)
+                newton_b(s)
 
         def rotate_part(s, odd):
             m = s // HEADS
@@ -234,7 +297,7 @@ def tile_grouped_query_key_scores_f1_kernel(
             nc.vector.scalar_tensor_tensor(
                 out=part[:].rearrange("p (i e) -> p i e", e=2),
                 in0=y_banks[s][:, odd:FEATURES:2].unsqueeze(2).to_broadcast([P, PAIRS, 2]),
-                scalar=r_tiles[s][:],
+                scalar=r_tiles[s],
                 in1=table[:].rearrange("p (i e) -> p i e", e=2),
                 op0=MULT,
                 op1=MULT,
@@ -301,42 +364,45 @@ def tile_grouped_query_key_scores_f1_kernel(
                 scale=1.0 / (CAP * math.sqrt(FEATURES)),
             )
 
-        def finish(s, j):
+        def finish(s, j, who):
             m, h = divmod(s, HEADS)
-            if j == 0:
+            rows = slice(m * P, (m + 1) * P)
+            if s not in results:
                 result = work.tile([P, KEYS], F32, name="result")
                 results[s] = result
-            rows = slice(m * P, (m + 1) * P)
             cols = slice(HALF * j, HALF * (j + 1))
             src, dst = tanh_tiles[s][:, cols], results[s][:, cols]
-            who = FINISH[j]
-            if s >= UNITS - 1:
-                who = "v"
-            if who == "v":
-                nc.vector.tensor_scalar(out=dst, in0=src, scalar1=CAP, scalar2=None, op0=MULT)
-            elif who == "g":
+            if who == "g":
                 nc.gpsimd.tensor_scalar(out=dst, in0=src, scalar1=CAP, scalar2=0.0, op0=MULT, op1=ADD)
-            else:
+            elif who == "s":
                 nc.scalar.activation(out=dst, in_=src, func=ACT.Copy, scale=CAP)
-            if s >= UNITS - 1:
-                nc.sync.dma_start(out=out[h, rows, cols], in_=dst)
-            elif j == 1:
-                nc.sync.dma_start(out=out[h, rows, :], in_=results[s][:])
+            else:
+                nc.vector.tensor_scalar(out=dst, in0=src, scalar1=CAP, scalar2=None, op0=MULT)
+            nc.sync.dma_start(out=out[h, rows, cols], in_=dst)
 
         widen_x("vector", 0, 0)
         widen_x("scalar", 0, 2)
         widen_x("vector", 0, 1)
         widen_x("scalar", 0, 3)
-        make_table(0, 0)
-        make_table(0, 1)
         x_banks = [
             transpose_x(0, 0, psum_z, "z"),
             transpose_x(0, 1, psum_z, "z"),
-            transpose_x(0, 2, psum_z, "z"),
-            transpose_x(0, 3, psum_t, "tx"),
+            transpose_x(0, 2, psum_y, "y"),
+            transpose_x(0, 3, psum_y, "y"),
         ]
-        for g in range(PASSES):
+        spread = psum_t.tile([P, 512], F32, name="tb")
+        nc.tensor.matmul(out=spread[:], lhsT=ones[:], rhs=gain_row[:], start=True, stop=True)
+        for g in range(2):
             widen_x("scalar", 1, g)
+        nc.scalar.copy(out=gain_all[:], in_=spread[:])
+        for g in range(2, 4):
+            widen_x("scalar", 1, g)
+        for e, sign in ((0, -1.0), (1, 1.0)):
+            nc.gpsimd.tensor_scalar(
+                out=gain_odd[:, :, e], in0=gain_all[:, 1:FEATURES:2], scalar1=sign, scalar2=0.0, op0=MULT, op1=ADD
+            )
+        make_table(0, 0)
+        make_table(0, 1)
         scale_x(0, 0, x_banks[0])
         scale_x(0, 1, x_banks[1])
         quantize_x(0, 0, 1)
@@ -344,76 +410,100 @@ def tile_grouped_query_key_scores_f1_kernel(
         quantize_x(0, 1, 2)
         scale_x(0, 3, x_banks[3])
         quantize_x(0, 2, 3)
-        y_first = transpose_x(1, 0, psum_t, "tb")
-        y_second = transpose_x(1, 1, psum_y, "y")
+        x_first = transpose_x(1, 0, psum_t, "tx")
+        x_second = transpose_x(1, 1, psum_y, "y")
         k_banks = [transpose_keys(0, 0, psum_z, "z"), transpose_keys(0, 1, psum_z, "z")]
         group_keys(0, 0, k_banks[0])
-        group_keys(0, 1, k_banks[1])
-        scale_x(1, 0, y_first)
+        scale_x(1, 0, x_first)
         quantize_x(0, 3, 4)
         project(0)
-        x_banks = [transpose_x(1, 2, psum_t, "tx"), transpose_x(1, 3, psum_y, "y")]
-        scale_x(1, 1, y_second)
+        x_banks = [transpose_x(1, 2, psum_t, "tx"), transpose_x(1, 3, psum_t, "tb")]
+        scale_x(1, 1, x_second)
         square(0)
-        k_banks = [transpose_keys(0, 2, psum_z, "z"), transpose_keys(0, 3, psum_z, "z")]
-        group_keys(0, 2, k_banks[0])
-        scale_x(1, 2, x_banks[0])
-        scale_x(1, 3, x_banks[1])
-        inverse_rms(0)
+        group_keys(0, 1, k_banks[1])
         project(1)
         square(1)
-        inverse_rms(1)
+        k_banks = [transpose_keys(0, 2, psum_z, "z"), transpose_keys(0, 3, psum_z, "z")]
+        scale_x(1, 2, x_banks[0])
+        half_mean(0)
+        scale_x(1, 3, x_banks[1])
+        first_guess(0)
+        newton(0, 3)
+        make_table(1, 0)
+        group_keys(0, 2, k_banks[0])
         group_keys(0, 3, k_banks[1])
+        quantize_x(1, 0, PASSES)
+        half_mean(1)
+        quantize_keys(0, 0)
+        first_guess(1)
+        newton(1, 3)
+        make_table(1, 1)
+        project(2)
+        square(2)
+        project(3)
+        key_quants = {0: ((0, 1),), 1: ((1, 0),), 2: ((1, 1),)}
 
-        pieces = {}
-        for m in range(2, M_TILES):
-            for g in range(PASSES):
-                pieces.setdefault(4 * m - 6 + g, []).append((m, g))
-        quants = {0: ((0, 0), (0, 1)), 1: ((1, 0),), 2: ((1, 1),)}
-
-        for s in range(UNITS + 2):
+        for s in range(UNITS + 3):
+            m, step = divmod(s + 8, 4)
+            products = [step] if 2 <= m < M_TILES and step < 2 else []
+            turns = [step - 1] if 2 <= m < M_TILES and step in (1, 2) else []
+            ready = s - 3 if 0 <= s - 3 < UNITS else None
+            if 0 < s < UNITS - 2:
+                first_guess(s + 2)
+                newton_a(s + 2)
+            if 1 <= s < 5:
+                make_table(2 + (s - 1) // 2, (s - 1) % 2)
+            if ready is not None:
+                for j in range(2):
+                    if finisher(ready, j) == "g":
+                        finish(ready, j, "g")
+            if 0 < s < UNITS - 2:
+                newton_b(s + 2)
+                newton(s + 2, 2)
+            if s + 3 < UNITS:
+                square(s + 3)
             if 0 <= s - 1 < UNITS:
                 transpose_b(s - 1)
-            now = pieces.get(s, [])
-            x_banks = [transpose_x(m, g, psum_t, "tx") for m, g in now]
-            if 0 <= s - 2 < UNITS:
-                cap_tanh(s - 2, 0)
+            x_banks = [turn_x(m, half) for half in turns]
             if 0 <= s - 1 < UNITS:
                 group_b(s - 1)
-            if 0 <= s - 2 < UNITS:
-                cap_tanh(s - 2, 1)
             if s < UNITS:
                 rotate_part(s, 0)
                 rotate_part(s, 1)
+            if ready is not None:
+                for j in range(2):
+                    if finisher(ready, j) == "v":
+                        finish(ready, j, "v")
+            if 0 <= s - 2 < UNITS:
+                score(s - 2, 0)
+                score(s - 2, 1)
+                cap_tanh(s - 2, 0)
+                cap_tanh(s - 2, 1)
             if s == 0:
-                quantize_x(1, 0, PASSES)
-            for bank, (m, g) in zip(x_banks, now):
-                scale_x(m, g, bank)
-            for g, j in quants.get(s, ()):
-                quantize_keys(g, j)
+                half_mean(2)
             if 0 <= s - 1 < UNITS:
                 quantize_b(s - 1)
             if s < UNITS:
                 rotate_add(s)
-            if 0 <= s - 2 < UNITS:
-                finish(s - 2, 0)
-                finish(s - 2, 1)
-            for m, g in now:
-                if g == PASSES - 1:
-                    quantize_x(m, 0, PASSES)
+            if s == 0:
+                first_guess(2)
+                newton(2, 3)
+            if s + 3 < UNITS:
+                half_mean(s + 3)
+            for g, j in key_quants.get(s, ()):
+                quantize_keys(g, j)
+            for half in products:
+                multiply_x(m, half)
+            for bank, half in zip(x_banks, turns):
+                group_x(m, half, bank)
+            if ready is not None:
+                for j in range(2):
+                    if finisher(ready, j) == "s":
+                        finish(ready, j, "s")
+            if 2 <= m < M_TILES and step == 3:
+                quantize_x(m, 0, PASSES)
             if s < 2:
                 for i in (2 * s, 2 * s + 1):
                     group_keys(1, i, transpose_keys(1, i, psum_z, "z"))
-            if s + 2 < UNITS:
-                project(s + 2)
-            if 0 <= s - 1 < UNITS:
-                score(s - 1, 0)
-                score(s - 1, 1)
-            if s + 2 < UNITS:
-                square(s + 2)
-            for m, g in pieces.get(s + 1, []):
-                widen_x("scalar", m, g)
-            if s + 2 < UNITS:
-                inverse_rms(s + 2)
-            if s // 2 + 1 < M_TILES:
-                make_table(s // 2 + 1, s % 2)
+            if s + 4 < UNITS:
+                project(s + 4)

@@ -20,6 +20,7 @@ FP8X4 = mybir.dt.float8_e4m3fn_x4
 FP4X4 = mybir.dt.float4_e2m1fn_x4
 MULT = mybir.AluOpType.mult
 ADD = mybir.AluOpType.add
+POW = mybir.AluOpType.pow
 ACT = mybir.ActivationFunctionType
 
 P = 128
@@ -28,15 +29,17 @@ M_TILES = TOKENS // P
 UNITS = M_TILES * HEADS
 HALF = KEYS // 2
 PAIRS = FEATURES // 2
-SEED_BITS = 0x5F3759DF - (1 << 22) - (1 << 30)
+
+TABLE_STEPS = {0: 1, 6: 2, 10: 3}
+X_STEPS = {1: (2, (0, 1)), 2: (2, (2,)), 3: (2, (3,)), 4: (3, (0,)), 5: (3, (1,)), 6: (3, (2,)), 7: (3, (3,))}
 
 
 def finisher(s, j):
-    if s >= 14:
+    if s % 2 == 1:
+        return "g"
+    if s >= UNITS - 4:
         return "v"
-    if s < 2:
-        return "vs"[j]
-    return "g" if j == 0 else "vs"[s % 2]
+    return "s" if s in (0, 2, 4, 6) else "vs"[j]
 
 
 def tile_grouped_query_key_scores_f1_kernel(
@@ -52,22 +55,21 @@ def tile_grouped_query_key_scores_f1_kernel(
         ctx.enter_context(tc.manual_schedule())
 
         ident = const.tile([P, P], F32, name="ident")
+        minus_half = const.tile([P, 2], F32, name="minus_half")
         warm = const.tile([P, 1], F32, name="warm")
         x_raw = [const.tile([P, CHANNELS], U8, name=f"x_raw{m}") for m in range(M_TILES)]
-        x_wide = const.tile([P, CHANNELS], F32, name="x_wide")
         x_factor = const.tile([P, PASSES, 4], F32, name="x_factor")
         w_codes = [const.tile([P, PASSES, 1024], U8, name=f"w_codes{h}", align_bytes=64) for h in range(HEADS)]
         w_scales = const.tile([P, PASSES, HEADS * FEATURES], U8, name="w_scales", align_bytes=64)
         k_raw = [const.tile([P, 8, FEATURES], BF16, name=f"k_raw{g}") for g in range(KEY_HEADS)]
         k_codes = [const.tile([P, KEYS], U32, name=f"k_codes{g}", align_bytes=64) for g in range(KEY_HEADS)]
         k_scales = [const.tile([P, KEYS], U8, name=f"k_scales{g}", align_bytes=64) for g in range(KEY_HEADS)]
-        trig = const.tile([P, M_TILES, 3, PAIRS], BF16, name="trig")
+        trig = const.tile([P, M_TILES, 2, PAIRS], BF16, name="trig")
         gain_row = const.tile([P, FEATURES], BF16, name="gain_row")
         ones = const.tile([P, P], BF16, name="ones")
-        gain_all = const.tile([P, FEATURES], F32, name="gain_all")
-        gain_odd = const.tile([P, PAIRS, 2], F32, name="gain_odd")
-        table_even = [const.tile([P, FEATURES], F32, name=f"table_even{m}") for m in range(M_TILES)]
-        table_odd = [const.tile([P, FEATURES], F32, name=f"table_odd{m}") for m in range(M_TILES)]
+        minus_ones = const.tile([P, P], BF16, name="minus_ones")
+        gains = const.tile([P, 2, PAIRS, 2], F32, name="gains")
+        table = [const.tile([P, 2, FEATURES], F32, name=f"table{m}") for m in range(M_TILES)]
         x_codes = [const.tile([P, PASSES, P], U32, name=f"x_codes{m}", align_bytes=64) for m in range(M_TILES)]
         x_scales = [const.tile([P, PASSES, P], U8, name=f"x_scales{m}", align_bytes=64) for m in range(M_TILES)]
         x_bf = [const.tile([P, CHANNELS], BF16, name=f"x_bf{m}") for m in range(M_TILES)]
@@ -92,17 +94,19 @@ def tile_grouped_query_key_scores_f1_kernel(
             )
 
         make_identity(nc, ident[:])
+        nc.gpsimd.memset(minus_half[:], -0.5)
         nc.vector.memset(warm[:], 0.0)
         nc.vector.memset(gain_row[:], 0.0)
         nc.vector.memset(ones[:], 1.0)
+        nc.vector.memset(minus_ones[:], -1.0)
         nc.vector.memset(w_scales[:].rearrange("p g n -> p (g n)").bitcast(I32), 0)
         load_x(0)
         nc.scalar.dma_start(out=x_factor[:], in_=x_scale.rearrange("o (g p t) -> p (o g) t", p=P, t=4))
         nc.scalar.dma_start(out=gain_row[0:1, :], in_=gain.unsqueeze(0))
-        for j, source in enumerate((cosines, sines, cosines)):
-            nc.scalar.dma_start(out=trig[:, 0, j, :], in_=source[0:P, :])
         nc.scalar.activation(out=warm[:], in_=warm[:], func=ACT.Tanh)
         load_x(1)
+        for j, source in enumerate((cosines, sines)):
+            nc.sync.dma_start(out=trig[:, :, j, :], in_=source.rearrange("(m p) i -> p m i", p=P))
         w_scales_i32 = w_scales[:].rearrange("p g n -> p (g n)").bitcast(I32).rearrange("p (g n) -> p g n", g=PASSES)
         wq_scales_i32 = wq_scales.bitcast(I32)
         for q in range(4):
@@ -113,31 +117,19 @@ def tile_grouped_query_key_scores_f1_kernel(
         load_w(0)
         load_keys(0, 0)
         load_w(1)
-        for j, source in enumerate((cosines, sines, cosines)):
-            nc.sync.dma_start(
-                out=trig[:, 1:M_TILES, j, :], in_=source[P:TOKENS, :].rearrange("(m p) i -> p m i", p=P)
-            )
         load_w(2)
         load_keys(0, 1)
         load_w(3)
-        load_keys(1, 0)
-        nc.sync.dma_start(out=x_wide[:], in_=x_scale.rearrange("o k -> (o k)").partition_broadcast(P))
         load_x(2)
+        load_keys(1, 0)
         load_keys(1, 1)
         load_x(3)
 
-        def make_table(m, odd, part=None):
-            pairs = slice(0, PAIRS) if part is None else slice(PAIRS // 2 * part, PAIRS // 2 * (part + 1))
-            n = pairs.stop - pairs.start
-            table = table_odd[m] if odd else table_even[m]
-            if odd:
-                factors = gain_odd[:, pairs, :]
-            else:
-                factors = gain_all[:, 2 * pairs.start : 2 * pairs.stop : 2].unsqueeze(2).to_broadcast([P, n, 2])
-            nc.gpsimd.tensor_tensor(
-                out=table[:].rearrange("p (i e) -> p i e", e=2)[:, pairs, :],
-                in0=trig[:, m, odd : odd + 2, pairs].rearrange("p e i -> p i e"),
-                in1=factors,
+        def make_table(m):
+            nc.vector.tensor_tensor(
+                out=table[m][:].rearrange("p q (i e) -> p q i e", e=2),
+                in0=trig[:, m].rearrange("p e i -> p i e").unsqueeze(1).to_broadcast([P, 2, PAIRS, 2]),
+                in1=gains[:],
                 op=MULT,
             )
 
@@ -149,19 +141,19 @@ def tile_grouped_query_key_scores_f1_kernel(
             else:
                 nc.scalar.copy(out=x_bf[m][:, cols], in_=src)
 
-        def transpose_x(m, g, pool, tag):
+        def transpose_x(m, groups, pool, tag):
             bank = pool.tile([P, 512], F32, name=tag)
             words = x_bf[m][:].bitcast(F32)
-            for u in range(2):
-                nc.tensor.transpose(
-                    bank[:, P * u : P * (u + 1)], words[:, 256 * g + u : 256 * (g + 1) : 2], ident[:]
-                )
+            for i, g in enumerate(groups):
+                for u in range(2):
+                    c = P * (2 * i + u)
+                    nc.tensor.transpose(bank[:, c : c + P], words[:, 256 * g + u : 256 * (g + 1) : 2], ident[:])
             return bank
 
-        def scale_x(m, g, bank):
+        def scale_x(m, g, bank, i=0):
             nc.vector.tensor_tensor(
                 out=x_grouped[m][:, g].rearrange("p r (u e) -> p r u e", u=2),
-                in0=bank[:, 0 : 2 * P].bitcast(BF16).rearrange("p (u r e) -> p r u e", u=2, e=2),
+                in0=bank[:, 2 * P * i : 2 * P * (i + 1)].bitcast(BF16).rearrange("p (u r e) -> p r u e", u=2, e=2),
                 in1=x_factor[:, g, :]
                 .rearrange("p (u e) -> p u e", u=2)
                 .unsqueeze(1)
@@ -174,31 +166,6 @@ def tile_grouped_query_key_scores_f1_kernel(
                 out=x_codes[m][:, g0:g1].rearrange("p g r -> p (g r)").bitcast(FP8X4),
                 scales=x_scales[m][:, g0:g1].rearrange("p g r -> p (g r)"),
                 in_=x_grouped[m][:, g0:g1].rearrange("p g r t -> p (g r t)"),
-            )
-
-        def multiply_x(m, half):
-            cols = slice(1024 * half, 1024 * (half + 1))
-            nc.vector.tensor_tensor(
-                out=x_bf[m][:, cols], in0=x_raw[m][:, cols].bitcast(FP8), in1=x_wide[:, cols], op=MULT
-            )
-
-        def turn_x(m, half):
-            bank = psum_t.tile([P, 512], F32, name="tx")
-            words = x_bf[m][:].bitcast(F32)
-            for g in (0, 1):
-                for u in (0, 1):
-                    first = 512 * half + 256 * g + u
-                    c = (2 * g + u) * P
-                    nc.tensor.transpose(bank[:, c : c + P], words[:, first : 512 * half + 256 * (g + 1) : 2], ident[:])
-            return bank
-
-        def group_x(m, half, bank):
-            nc.scalar.copy(
-                out=x_grouped[m][:, 2 * half : 2 * half + 2]
-                .rearrange("p g r t -> p (g r t)")
-                .bitcast(F32)
-                .rearrange("p (g r u) -> p g r u", g=2, u=2),
-                in_=bank[:].rearrange("p (g u r) -> p g r u", g=2, u=2),
             )
 
         def transpose_keys(g, i, pool, tag):
@@ -228,7 +195,7 @@ def tile_grouped_query_key_scores_f1_kernel(
                 in_=k_grouped[g][j][:].rearrange("p r t -> p (r t)"),
             )
 
-        results, change_tiles, half_tiles, y_banks, r_tiles, p_tiles, b_tiles, bt_tiles, bq_tiles, z_banks, tanh_tiles = {}, {}, {}, {}, {}, {}, {}, {}, {}, {}, {}
+        results, total_tiles, mean_tiles, y_banks, r_tiles, p_tiles, b_tiles, bt_tiles, bq_tiles, z_banks, tanh_tiles = {}, {}, {}, {}, {}, {}, {}, {}, {}, {}, {}
 
         def project(s):
             m, h = divmod(s, HEADS)
@@ -247,58 +214,47 @@ def tile_grouped_query_key_scores_f1_kernel(
 
         def square(s):
             junk = work.tile([P, FEATURES], BF16, name="junk")
-            total = work.tile([P, 1], F32, name="total", bufs=6)
-            nc.scalar.activation(out=junk[:], in_=y_banks[s][:], func=ACT.Square, accum_out=total[:])
-            r_tiles[s] = total
-
-        def half_mean(s):
-            half = work.tile([P, 1], F32, name="half", bufs=6)
-            nc.vector.tensor_scalar(
-                out=half[:], in0=r_tiles[s][:], scalar1=-0.5 / FEATURES, scalar2=-0.5 * EPS, op0=MULT, op1=ADD
+            if s % 2 == 0:
+                total = work.tile([P, 2], F32, name="total", bufs=4)
+                total_tiles[s // 2] = total
+            nc.scalar.activation(
+                out=junk[:],
+                in_=y_banks[s][:],
+                func=ACT.Square,
+                accum_out=total_tiles[s // 2][:, s % 2 : s % 2 + 1],
             )
-            half_tiles[s] = half
 
-        def first_guess(s):
-            seed = work.tile([P, 1], I32, name="seed", bufs=6)
+        def mean_square(units):
+            n = len(units)
+            mean = work.tile([P, 2], F32, name="mean")
+            first = units[0] % 2
             nc.vector.tensor_scalar(
-                out=seed[:],
-                in0=half_tiles[s][:].bitcast(I32),
-                scalar1=-0.5,
-                scalar2=float(SEED_BITS),
+                out=mean[:, 0:n],
+                in0=total_tiles[units[0] // 2][:, first : first + n],
+                scalar1=1.0 / FEATURES,
+                scalar2=EPS,
                 op0=MULT,
                 op1=ADD,
             )
-            r_tiles[s] = seed[:].bitcast(F32)
+            mean_tiles[units[0]] = mean
 
-        def newton_a(s):
-            guess = r_tiles[s]
-            change = work.tile([P, 1], F32, name="change", bufs=6)
-            nc.gpsimd.tensor_scalar(
-                out=change[:], in0=guess, scalar1=guess, scalar2=half_tiles[s][:], op0=MULT, op1=MULT
+        def inverse_root(units):
+            n = len(units)
+            root = work.tile([P, 2], F32, name="root", bufs=4)
+            nc.gpsimd.tensor_tensor(
+                out=root[:, 0:n], in0=mean_tiles[units[0]][:, 0:n], in1=minus_half[:, 0:n], op=POW
             )
-            change_tiles[s] = change
-
-        def newton_b(s):
-            better = work.tile([P, 1], F32, name="better", bufs=12)
-            nc.gpsimd.tensor_scalar(
-                out=better[:], in0=change_tiles[s][:], scalar1=1.5, scalar2=r_tiles[s], op0=ADD, op1=MULT
-            )
-            r_tiles[s] = better[:]
-
-        def newton(s, steps):
-            for i in range(steps):
-                newton_a(s)
-                newton_b(s)
+            for i, s in enumerate(units):
+                r_tiles[s] = root[:, i : i + 1]
 
         def rotate_part(s, odd):
             m = s // HEADS
             part = work.tile([P, FEATURES], F32, name="part_odd" if odd else "part_even")
-            table = table_odd[m] if odd else table_even[m]
             nc.vector.scalar_tensor_tensor(
                 out=part[:].rearrange("p (i e) -> p i e", e=2),
                 in0=y_banks[s][:, odd:FEATURES:2].unsqueeze(2).to_broadcast([P, PAIRS, 2]),
                 scalar=r_tiles[s],
-                in1=table[:].rearrange("p (i e) -> p i e", e=2),
+                in1=table[m][:, odd].rearrange("p (i e) -> p i e", e=2),
                 op0=MULT,
                 op1=MULT,
             )
@@ -309,7 +265,7 @@ def tile_grouped_query_key_scores_f1_kernel(
             nc.vector.tensor_tensor(
                 out=b[:].rearrange("p (u k e) -> p u k e", u=2, e=2),
                 in0=p_tiles[s, 0][:].rearrange("p (k u e) -> p u k e", u=2, e=2),
-                in1=p_tiles[s, 1][:].rearrange("p (k u e) -> p u k e", u=2, e=2),
+                in1=p_tiles[s, 1][:].rearrange("p (k u e) -> p u k e", u=2, e=2)[:, :, :, ::-1],
                 op=ADD,
             )
             b_tiles[s] = b
@@ -373,7 +329,12 @@ def tile_grouped_query_key_scores_f1_kernel(
             cols = slice(HALF * j, HALF * (j + 1))
             src, dst = tanh_tiles[s][:, cols], results[s][:, cols]
             if who == "g":
-                nc.gpsimd.tensor_scalar(out=dst, in0=src, scalar1=CAP, scalar2=0.0, op0=MULT, op1=ADD)
+                dst, src = results[s][:], tanh_tiles[s][:]
+                cap = work.tile([P, 1], F32, name="cap")
+                nc.vector.memset(cap[:], CAP)
+                nc.gpsimd.tensor_scalar(out=dst, in0=src, scalar1=cap[:], scalar2=0.0, op0=MULT, op1=ADD)
+                nc.sync.dma_start(out=out[h, rows, :], in_=dst)
+                return
             elif who == "s":
                 nc.scalar.activation(out=dst, in_=src, func=ACT.Copy, scale=CAP)
             else:
@@ -385,24 +346,27 @@ def tile_grouped_query_key_scores_f1_kernel(
         widen_x("vector", 0, 1)
         widen_x("scalar", 0, 3)
         x_banks = [
-            transpose_x(0, 0, psum_z, "z"),
-            transpose_x(0, 1, psum_z, "z"),
-            transpose_x(0, 2, psum_y, "y"),
-            transpose_x(0, 3, psum_y, "y"),
+            transpose_x(0, (0,), psum_z, "z"),
+            transpose_x(0, (1,), psum_z, "z"),
+            transpose_x(0, (2,), psum_y, "y"),
+            transpose_x(0, (3,), psum_y, "y"),
         ]
-        spread = psum_t.tile([P, 512], F32, name="tb")
-        nc.tensor.matmul(out=spread[:], lhsT=ones[:], rhs=gain_row[:], start=True, stop=True)
+        gain_banks = [psum_t.tile([P, 512], F32, name="tb"), psum_t.tile([P, 512], F32, name="tx")]
+        for q in range(2):
+            for e in range(2):
+                nc.tensor.matmul(
+                    out=gain_banks[q][:, e : 2 * PAIRS : 2],
+                    lhsT=(minus_ones if q == 1 and e == 1 else ones)[:],
+                    rhs=gain_row[:, q : 2 * PAIRS : 2],
+                    start=True,
+                    stop=True,
+                )
         for g in range(2):
             widen_x("scalar", 1, g)
-        nc.scalar.copy(out=gain_all[:], in_=spread[:])
+        for q in range(2):
+            nc.scalar.copy(out=gains[:, q].rearrange("p i e -> p (i e)"), in_=gain_banks[q][:])
         for g in range(2, 4):
             widen_x("scalar", 1, g)
-        for e, sign in ((0, -1.0), (1, 1.0)):
-            nc.gpsimd.tensor_scalar(
-                out=gain_odd[:, :, e], in0=gain_all[:, 1:FEATURES:2], scalar1=sign, scalar2=0.0, op0=MULT, op1=ADD
-            )
-        make_table(0, 0)
-        make_table(0, 1)
         scale_x(0, 0, x_banks[0])
         scale_x(0, 1, x_banks[1])
         quantize_x(0, 0, 1)
@@ -410,100 +374,100 @@ def tile_grouped_query_key_scores_f1_kernel(
         quantize_x(0, 1, 2)
         scale_x(0, 3, x_banks[3])
         quantize_x(0, 2, 3)
-        x_first = transpose_x(1, 0, psum_t, "tx")
-        x_second = transpose_x(1, 1, psum_y, "y")
-        k_banks = [transpose_keys(0, 0, psum_z, "z"), transpose_keys(0, 1, psum_z, "z")]
-        group_keys(0, 0, k_banks[0])
-        scale_x(1, 0, x_first)
+        x1_banks = [transpose_x(1, (0,), psum_t, "tx"), transpose_x(1, (1,), psum_y, "y")]
         quantize_x(0, 3, 4)
         project(0)
-        x_banks = [transpose_x(1, 2, psum_t, "tx"), transpose_x(1, 3, psum_t, "tb")]
-        scale_x(1, 1, x_second)
+        make_table(0)
         square(0)
-        group_keys(0, 1, k_banks[1])
         project(1)
         square(1)
-        k_banks = [transpose_keys(0, 2, psum_z, "z"), transpose_keys(0, 3, psum_z, "z")]
-        scale_x(1, 2, x_banks[0])
-        half_mean(0)
-        scale_x(1, 3, x_banks[1])
-        first_guess(0)
-        newton(0, 3)
-        make_table(1, 0)
-        group_keys(0, 2, k_banks[0])
-        group_keys(0, 3, k_banks[1])
-        quantize_x(1, 0, PASSES)
-        half_mean(1)
-        quantize_keys(0, 0)
-        first_guess(1)
-        newton(1, 3)
-        make_table(1, 1)
+        scale_x(1, 0, x1_banks[0])
+        scale_x(1, 1, x1_banks[1])
+        mean_square((0,))
+        inverse_root((0,))
+        x1_banks += [transpose_x(1, (2,), psum_t, "tb"), transpose_x(1, (3,), psum_t, "tx")]
+        k_banks = [transpose_keys(0, 0, psum_z, "z"), transpose_keys(0, 1, psum_z, "z")]
+        group_keys(0, 0, k_banks[0])
+        group_keys(0, 1, k_banks[1])
+        scale_x(1, 2, x1_banks[2])
+        scale_x(1, 3, x1_banks[3])
+        mean_square((1,))
+        inverse_root((1,))
         project(2)
         square(2)
-        project(3)
-        key_quants = {0: ((0, 1),), 1: ((1, 0),), 2: ((1, 1),)}
+        k_banks = [transpose_keys(0, 2, psum_z, "z"), transpose_keys(0, 3, psum_z, "z")]
+        group_keys(0, 2, k_banks[0])
+        group_keys(0, 3, k_banks[1])
+        key_quants = {2: ((1, 0),), 3: ((1, 1),)}
 
-        for s in range(UNITS + 3):
-            m, step = divmod(s + 8, 4)
-            products = [step] if 2 <= m < M_TILES and step < 2 else []
-            turns = [step - 1] if 2 <= m < M_TILES and step in (1, 2) else []
-            ready = s - 3 if 0 <= s - 3 < UNITS else None
-            if 0 < s < UNITS - 2:
-                first_guess(s + 2)
-                newton_a(s + 2)
-            if 1 <= s < 5:
-                make_table(2 + (s - 1) // 2, (s - 1) % 2)
-            if ready is not None:
-                for j in range(2):
-                    if finisher(ready, j) == "g":
-                        finish(ready, j, "g")
-            if 0 < s < UNITS - 2:
-                newton_b(s + 2)
-                newton(s + 2, 2)
+        for s in range(UNITS):
+            m, groups = X_STEPS.get(s, (0, ()))
+            if s % 2 == 1 and s + 2 < UNITS:
+                mean_square((s + 1, s + 2))
+                inverse_root((s + 1, s + 2))
+            if s >= 3 and finisher(s - 3, 0) == "g":
+                finish(s - 3, 0, "g")
+            next_m, next_groups = X_STEPS.get(s + 1, (0, ()))
+            for g in next_groups:
+                widen_x("scalar", next_m, g)
             if s + 3 < UNITS:
+                project(s + 3)
                 square(s + 3)
-            if 0 <= s - 1 < UNITS:
+            if s >= 1:
                 transpose_b(s - 1)
-            x_banks = [turn_x(m, half) for half in turns]
-            if 0 <= s - 1 < UNITS:
+            if groups:
+                x_bank = transpose_x(m, groups, psum_t, "tx")
+            if s >= 1:
                 group_b(s - 1)
-            if s < UNITS:
-                rotate_part(s, 0)
-                rotate_part(s, 1)
-            if ready is not None:
-                for j in range(2):
-                    if finisher(ready, j) == "v":
-                        finish(ready, j, "v")
-            if 0 <= s - 2 < UNITS:
+            rotate_part(s, 0)
+            rotate_part(s, 1)
+            if s == 1:
+                quantize_keys(0, 1)
+            for i, g in enumerate(groups):
+                scale_x(m, g, x_bank, i)
+            if s == 0:
+                quantize_x(1, 0, PASSES)
+                quantize_keys(0, 0)
+            if s >= 2:
                 score(s - 2, 0)
                 score(s - 2, 1)
                 cap_tanh(s - 2, 0)
                 cap_tanh(s - 2, 1)
-            if s == 0:
-                half_mean(2)
-            if 0 <= s - 1 < UNITS:
+            for j in range(2):
+                if s >= 3 and finisher(s - 3, j) == "v":
+                    finish(s - 3, j, "v")
+            if s == UNITS - 1:
                 quantize_b(s - 1)
-            if s < UNITS:
-                rotate_add(s)
-            if s == 0:
-                first_guess(2)
-                newton(2, 3)
-            if s + 3 < UNITS:
-                half_mean(s + 3)
+            rotate_add(s)
             for g, j in key_quants.get(s, ()):
                 quantize_keys(g, j)
-            for half in products:
-                multiply_x(m, half)
-            for bank, half in zip(x_banks, turns):
-                group_x(m, half, bank)
-            if ready is not None:
-                for j in range(2):
-                    if finisher(ready, j) == "s":
-                        finish(ready, j, "s")
-            if 2 <= m < M_TILES and step == 3:
+            if s in TABLE_STEPS:
+                make_table(TABLE_STEPS[s])
+            for j in range(2):
+                if s >= 3 and finisher(s - 3, j) == "s":
+                    finish(s - 3, j, "s")
+            if PASSES - 1 in groups:
                 quantize_x(m, 0, PASSES)
+            if 0 < s < UNITS - 1:
+                quantize_b(s - 1)
             if s < 2:
                 for i in (2 * s, 2 * s + 1):
                     group_keys(1, i, transpose_keys(1, i, psum_z, "z"))
-            if s + 4 < UNITS:
-                project(s + 4)
+
+        last = UNITS - 1
+        finish(last - 2, 0, "g")
+        score(last - 1, 0)
+        score(last - 1, 1)
+        transpose_b(last)
+        cap_tanh(last - 1, 0)
+        group_b(last)
+        cap_tanh(last - 1, 1)
+        quantize_b(last)
+        finish(last - 1, 0, "v")
+        score(last, 0)
+        score(last, 1)
+        cap_tanh(last, 0)
+        finish(last - 1, 1, "v")
+        cap_tanh(last, 1)
+        finish(last, 0, "v")
+        finish(last, 1, "v")

@@ -64,7 +64,7 @@ def tile_grouped_query_key_scores_f1_kernel(
         k_raw = [const.tile([P, 8, FEATURES], BF16, name=f"k_raw{g}") for g in range(KEY_HEADS)]
         k_codes = [const.tile([P, KEYS], U32, name=f"k_codes{g}", align_bytes=64) for g in range(KEY_HEADS)]
         k_scales = [const.tile([P, KEYS], U8, name=f"k_scales{g}", align_bytes=64) for g in range(KEY_HEADS)]
-        trig = const.tile([P, M_TILES, 2, PAIRS], BF16, name="trig")
+        trig = const.tile([P, M_TILES, 3, PAIRS], BF16, name="trig")
         gain_row = const.tile([P, FEATURES], BF16, name="gain_row")
         ones = const.tile([P, P], BF16, name="ones")
         minus_ones = const.tile([P, P], BF16, name="minus_ones")
@@ -89,8 +89,8 @@ def tile_grouped_query_key_scores_f1_kernel(
 
         def load_keys(g, j):
             nc.sync.dma_start(
-                out=k_raw[g][:, 4 * j : 4 * j + 4, :].rearrange("p (n i) d -> p n (i d)", i=2),
-                in_=keys[g, HALF * j : HALF * (j + 1), :].rearrange("(n p i) d -> p n (i d)", p=P, i=2),
+                out=k_raw[g][:, 4 * j : 4 * j + 4, :],
+                in_=keys[g, HALF * j : HALF * (j + 1), :].rearrange("(n p) d -> p n d", p=P),
             )
 
         make_identity(nc, ident[:])
@@ -126,12 +126,14 @@ def tile_grouped_query_key_scores_f1_kernel(
         load_x(3)
 
         def make_table(m):
-            nc.vector.tensor_tensor(
-                out=table[m][:].rearrange("p q (i e) -> p q i e", e=2),
-                in0=trig[:, m].rearrange("p e i -> p i e").unsqueeze(1).to_broadcast([P, 2, PAIRS, 2]),
-                in1=gains[:],
-                op=MULT,
-            )
+            nc.vector.tensor_copy(out=trig[:, m, 2, :], in_=trig[:, m, 0, :])
+            for q in range(2):
+                nc.vector.tensor_tensor(
+                    out=table[m][:, q].rearrange("p (i e) -> p i e", e=2),
+                    in0=trig[:, m, q : q + 2].rearrange("p e i -> p i e"),
+                    in1=gains[:, q],
+                    op=MULT,
+                )
 
         def widen_x(engine, m, g):
             cols = slice(512 * g, 512 * (g + 1))
@@ -183,8 +185,8 @@ def tile_grouped_query_key_scores_f1_kernel(
                 out=k_grouped[g][i // 2][:, c : c + 256, :]
                 .rearrange("p r t -> p (r t)")
                 .bitcast(F32)
-                .rearrange("p (r c) -> p r c", c=4),
-                in_=bank[:].rearrange("p (c r) -> p r c", c=4),
+                .rearrange("p (n r u) -> p n r u", n=2, u=2),
+                in_=bank[:].rearrange("p (n u r) -> p n r u", n=2, u=2),
             )
 
         def quantize_keys(g, j):
@@ -262,19 +264,14 @@ def tile_grouped_query_key_scores_f1_kernel(
 
         def rotate_add(s):
             b = work.tile([P, FEATURES], BF16, name="b")
-            nc.vector.tensor_tensor(
-                out=b[:].rearrange("p (u k e) -> p u k e", u=2, e=2),
-                in0=p_tiles[s, 0][:].rearrange("p (k u e) -> p u k e", u=2, e=2),
-                in1=p_tiles[s, 1][:].rearrange("p (k u e) -> p u k e", u=2, e=2)[:, :, :, ::-1],
-                op=ADD,
-            )
+            nc.vector.tensor_tensor(out=b[:], in0=p_tiles[s, 0][:], in1=p_tiles[s, 1][:], op=ADD)
             b_tiles[s] = b
 
         def transpose_b(s):
             bank = psum_t.tile([P, 512], F32, name="tb")
             words = b_tiles[s][:].bitcast(F32)
             for u in range(2):
-                nc.tensor.transpose(bank[:, P * u : P * (u + 1)], words[:, P * u : P * (u + 1)], ident[:])
+                nc.tensor.transpose(bank[:, P * u : P * (u + 1)], words[:, u : 2 * P : 2], ident[:])
             bt_tiles[s] = bank
 
         def group_b(s):
@@ -356,7 +353,7 @@ def tile_grouped_query_key_scores_f1_kernel(
             for e in range(2):
                 nc.tensor.matmul(
                     out=gain_banks[q][:, e : 2 * PAIRS : 2],
-                    lhsT=(minus_ones if q == 1 and e == 1 else ones)[:],
+                    lhsT=(minus_ones if q == 1 and e == 0 else ones)[:],
                     rhs=gain_row[:, q : 2 * PAIRS : 2],
                     start=True,
                     stop=True,

import math
from contextlib import ExitStack

import concourse.mybir as mybir
from concourse.masks import make_identity

TOKENS, CHANNELS, HEADS, KEY_HEADS, FEATURES, KEYS = 512, 2048, 4, 2, 512, 1024
EPS = 0.05
CAP = 5.0

FLOPS = 2 * TOKENS * CHANNELS * HEADS * FEATURES + 2 * HEADS * TOKENS * KEYS * FEATURES

F32 = mybir.dt.float32
BF16 = mybir.dt.bfloat16
I32 = mybir.dt.int32
U32 = mybir.dt.uint32
U8 = mybir.dt.uint8
FP8 = mybir.dt.float8_e4m3fn
FP8X4 = mybir.dt.float8_e4m3fn_x4
FP4X4 = mybir.dt.float4_e2m1fn_x4
MULT = mybir.AluOpType.mult
ADD = mybir.AluOpType.add
POW = mybir.AluOpType.pow
ACT = mybir.ActivationFunctionType

P = 128
PASSES = CHANNELS // 512
M_TILES = TOKENS // P
UNITS = M_TILES * HEADS
HALF = KEYS // 2
PAIRS = FEATURES // 2

TABLE_STEPS = {0: 1, 6: 2, 10: 3}
X_STEPS = {1: (2, (0, 1)), 2: (2, (2,)), 3: (2, (3,)), 4: (3, (0,)), 5: (3, (1,)), 6: (3, (2,)), 7: (3, (3,))}


def finisher(s, j):
    if s % 2 == 1:
        return "g"
    if s >= UNITS - 4:
        return "v"
    return "s" if s in (0, 2, 4, 6) else "vs"[j]


def tile_grouped_query_key_scores_f1_kernel(
    tc, x_bytes, x_scale, wq_words, wq_scales, gain, cosines, sines, keys, out
):
    nc = tc.nc
    with ExitStack() as ctx:
        const = ctx.enter_context(tc.tile_pool(name="const", bufs=1))
        work = ctx.enter_context(tc.tile_pool(name="work", bufs=3))
        psum_y = ctx.enter_context(tc.psum_pool(name="psum_y", bufs=4))
        psum_z = ctx.enter_context(tc.psum_pool(name="psum_z", bufs=2))
        psum_t = ctx.enter_context(tc.psum_pool(name="psum_t", bufs=1))
        ctx.enter_context(tc.manual_schedule())

        ident = const.tile([P, P], F32, name="ident")
        minus_half = const.tile([P, 2], F32, name="minus_half")
        warm = const.tile([P, 1], F32, name="warm")
        x_raw = [const.tile([P, CHANNELS], U8, name=f"x_raw{m}") for m in range(M_TILES)]
        x_factor = const.tile([P, PASSES, 4], F32, name="x_factor")
        w_codes = [const.tile([P, PASSES, 1024], U8, name=f"w_codes{h}", align_bytes=64) for h in range(HEADS)]
        w_scales = const.tile([P, PASSES, HEADS * FEATURES], U8, name="w_scales", align_bytes=64)
        k_raw = [const.tile([P, 8, FEATURES], BF16, name=f"k_raw{g}") for g in range(KEY_HEADS)]
        k_codes = [const.tile([P, KEYS], U32, name=f"k_codes{g}", align_bytes=64) for g in range(KEY_HEADS)]
        k_scales = [const.tile([P, KEYS], U8, name=f"k_scales{g}", align_bytes=64) for g in range(KEY_HEADS)]
        trig = const.tile([P, M_TILES, 3, PAIRS], BF16, name="trig")
        gain_row = const.tile([P, FEATURES], BF16, name="gain_row")
        ones = const.tile([P, P], BF16, name="ones")
        minus_ones = const.tile([P, P], BF16, name="minus_ones")
        gains = const.tile([P, 2, PAIRS, 2], F32, name="gains")
        table = [const.tile([P, 2, FEATURES], F32, name=f"table{m}") for m in range(M_TILES)]
        x_codes = [const.tile([P, PASSES, P], U32, name=f"x_codes{m}", align_bytes=64) for m in range(M_TILES)]
        x_scales = [const.tile([P, PASSES, P], U8, name=f"x_scales{m}", align_bytes=64) for m in range(M_TILES)]
        x_bf = [const.tile([P, CHANNELS], BF16, name=f"x_bf{m}") for m in range(M_TILES)]
        x_grouped = [const.tile([P, PASSES, P, 4], BF16, name=f"x_grouped{m}", align_bytes=64) for m in range(M_TILES)]
        k_grouped = [
            [const.tile([P, HALF, 4], BF16, name=f"k_grouped{g}{j}", align_bytes=64) for j in range(2)]
            for g in range(KEY_HEADS)
        ]

        def load_x(m):
            nc.sync.dma_start(out=x_raw[m][:], in_=x_bytes[m * P : (m + 1) * P, :])

        def load_w(h):
            nc.sync.dma_start(
                out=w_codes[h][:], in_=wq_words[:, :, 1024 * h : 1024 * (h + 1)].rearrange("g p b -> p g b")
            )

        def load_keys(g, j):
            nc.sync.dma_start(
                out=k_raw[g][:, 4 * j : 4 * j + 4, :],
                in_=keys[g, HALF * j : HALF * (j + 1), :].rearrange("(n p) d -> p n d", p=P),
            )

        make_identity(nc, ident[:])
        nc.gpsimd.memset(minus_half[:], -0.5)
        nc.vector.memset(warm[:], 0.0)
        nc.vector.memset(gain_row[:], 0.0)
        nc.vector.memset(ones[:], 1.0)
        nc.vector.memset(minus_ones[:], -1.0)
        nc.vector.memset(w_scales[:].rearrange("p g n -> p (g n)").bitcast(I32), 0)
        load_x(0)
        nc.scalar.dma_start(out=x_factor[:], in_=x_scale.rearrange("o (g p t) -> p (o g) t", p=P, t=4))
        nc.scalar.dma_start(out=gain_row[0:1, :], in_=gain.unsqueeze(0))
        nc.scalar.activation(out=warm[:], in_=warm[:], func=ACT.Tanh)
        load_x(1)
        for j, source in enumerate((cosines, sines)):
            nc.sync.dma_start(out=trig[:, :, j, :], in_=source.rearrange("(m p) i -> p m i", p=P))
        w_scales_i32 = w_scales[:].rearrange("p g n -> p (g n)").bitcast(I32).rearrange("p (g n) -> p g n", g=PASSES)
        wq_scales_i32 = wq_scales.bitcast(I32)
        for q in range(4):
            nc.sync.dma_start(
                out=w_scales_i32[32 * q : 32 * q + 4],
                in_=wq_scales_i32[:, 4 * q : 4 * q + 4, :].rearrange("g q n -> q g n"),
            )
        load_w(0)
        load_keys(0, 0)
        load_w(1)
        load_w(2)
        load_keys(0, 1)
        load_w(3)
        load_x(2)
        load_keys(1, 0)
        load_keys(1, 1)
        load_x(3)

        def make_table(m):
            nc.vector.tensor_copy(out=trig[:, m, 2, :], in_=trig[:, m, 0, :])
            for q in range(2):
                nc.vector.tensor_tensor(
                    out=table[m][:, q].rearrange("p (i e) -> p i e", e=2),
                    in0=trig[:, m, q : q + 2].rearrange("p e i -> p i e"),
                    in1=gains[:, q],
                    op=MULT,
                )

        def widen_x(engine, m, g):
            cols = slice(512 * g, 512 * (g + 1))
            src = x_raw[m][:, cols].bitcast(FP8)
            if engine == "vector":
                nc.vector.tensor_copy(out=x_bf[m][:, cols], in_=src)
            else:
                nc.scalar.copy(out=x_bf[m][:, cols], in_=src)

        def transpose_x(m, groups, pool, tag):
            bank = pool.tile([P, 512], F32, name=tag)
            words = x_bf[m][:].bitcast(F32)
            for i, g in enumerate(groups):
                for u in range(2):
                    c = P * (2 * i + u)
                    nc.tensor.transpose(bank[:, c : c + P], words[:, 256 * g + u : 256 * (g + 1) : 2], ident[:])
            return bank

        def scale_x(m, g, bank, i=0):
            nc.vector.tensor_tensor(
                out=x_grouped[m][:, g].rearrange("p r (u e) -> p r u e", u=2),
                in0=bank[:, 2 * P * i : 2 * P * (i + 1)].bitcast(BF16).rearrange("p (u r e) -> p r u e", u=2, e=2),
                in1=x_factor[:, g, :]
                .rearrange("p (u e) -> p u e", u=2)
                .unsqueeze(1)
                .to_broadcast([P, P, 2, 2]),
                op=MULT,
            )

        def quantize_x(m, g0, g1):
            nc.vector.quantize_mx(
                out=x_codes[m][:, g0:g1].rearrange("p g r -> p (g r)").bitcast(FP8X4),
                scales=x_scales[m][:, g0:g1].rearrange("p g r -> p (g r)"),
                in_=x_grouped[m][:, g0:g1].rearrange("p g r t -> p (g r t)"),
            )

        def transpose_keys(g, i, pool, tag):
            bank = pool.tile([P, 512], F32, name=tag)
            for n in range(2):
                words = k_raw[g][:, 2 * i + n, :].bitcast(F32)
                for u in range(2):
                    c = (2 * n + u) * P
                    nc.tensor.transpose(bank[:, c : c + P], words[:, u:256:2], ident[:])
            return bank

        def group_keys(g, i, bank):
            c = 256 * (i % 2)
            nc.scalar.copy(
                out=k_grouped[g][i // 2][:, c : c + 256, :]
                .rearrange("p r t -> p (r t)")
                .bitcast(F32)
                .rearrange("p (n r u) -> p n r u", n=2, u=2),
                in_=bank[:].rearrange("p (n u r) -> p n r u", n=2, u=2),
            )

        def quantize_keys(g, j):
            cols = slice(HALF * j, HALF * (j + 1))
            nc.vector.quantize_mx(
                out=k_codes[g][:, cols].bitcast(FP8X4),
                scales=k_scales[g][:, cols],
                in_=k_grouped[g][j][:].rearrange("p r t -> p (r t)"),
            )

        results, total_tiles, mean_tiles, y_banks, r_tiles, p_tiles, b_tiles, bt_tiles, bq_tiles, z_banks, tanh_tiles = {}, {}, {}, {}, {}, {}, {}, {}, {}, {}, {}

        def project(s):
            m, h = divmod(s, HEADS)
            y = psum_y.tile([P, 512], F32, name="y")
            for g in range(PASSES):
                nc.tensor.matmul_mx(
                    out=y[:],
                    lhsT=x_codes[m][:, g, :].bitcast(FP8X4),
                    lhsT_scale=x_scales[m][:, g, :],
                    rhs=w_codes[h][:, g, :].bitcast(FP4X4),
                    rhs_scale=w_scales[:, g, FEATURES * h : FEATURES * (h + 1)],
                    start=(g == 0),
                    stop=(g == PASSES - 1),
                )
            y_banks[s] = y

        def square(s):
            junk = work.tile([P, FEATURES], BF16, name="junk")
            if s % 2 == 0:
                total = work.tile([P, 2], F32, name="total", bufs=4)
                total_tiles[s // 2] = total
            nc.scalar.activation(
                out=junk[:],
                in_=y_banks[s][:],
                func=ACT.Square,
                accum_out=total_tiles[s // 2][:, s % 2 : s % 2 + 1],
            )

        def mean_square(units):
            n = len(units)
            mean = work.tile([P, 2], F32, name="mean")
            first = units[0] % 2
            nc.vector.tensor_scalar(
                out=mean[:, 0:n],
                in0=total_tiles[units[0] // 2][:, first : first + n],
                scalar1=1.0 / FEATURES,
                scalar2=EPS,
                op0=MULT,
                op1=ADD,
            )
            mean_tiles[units[0]] = mean

        def inverse_root(units):
            n = len(units)
            root = work.tile([P, 2], F32, name="root", bufs=4)
            nc.gpsimd.tensor_tensor(
                out=root[:, 0:n], in0=mean_tiles[units[0]][:, 0:n], in1=minus_half[:, 0:n], op=POW
            )
            for i, s in enumerate(units):
                r_tiles[s] = root[:, i : i + 1]

        def rotate_part(s, odd):
            m = s // HEADS
            part = work.tile([P, FEATURES], F32, name="part_odd" if odd else "part_even")
            nc.vector.scalar_tensor_tensor(
                out=part[:].rearrange("p (i e) -> p i e", e=2),
                in0=y_banks[s][:, odd:FEATURES:2].unsqueeze(2).to_broadcast([P, PAIRS, 2]),
                scalar=r_tiles[s],
                in1=table[m][:, odd].rearrange("p (i e) -> p i e", e=2),
                op0=MULT,
                op1=MULT,
            )
            p_tiles[s, odd] = part

        def rotate_add(s):
            b = work.tile([P, FEATURES], BF16, name="b")
            nc.vector.tensor_tensor(out=b[:], in0=p_tiles[s, 0][:], in1=p_tiles[s, 1][:], op=ADD)
            b_tiles[s] = b

        def transpose_b(s):
            bank = psum_t.tile([P, 512], F32, name="tb")
            words = b_tiles[s][:].bitcast(F32)
            for u in range(2):
                nc.tensor.transpose(bank[:, P * u : P * (u + 1)], words[:, u : 2 * P : 2], ident[:])
            bt_tiles[s] = bank

        def group_b(s):
            grouped = work.tile([P, P, 4], BF16, name="b_grouped", align_bytes=64)
            nc.scalar.copy(
                out=grouped[:].rearrange("p r t -> p (r t)").bitcast(F32).rearrange("p (r u) -> p r u", u=2),
                in_=bt_tiles[s][:, 0 : 2 * P].rearrange("p (u r) -> p r u", u=2),
            )
            bt_tiles[s] = grouped

        def quantize_b(s):
            codes = work.tile([P, P], U32, name="b_codes", align_bytes=64)
            scales = work.tile([P, P], U8, name="b_scales", align_bytes=64)
            nc.vector.quantize_mx(
                out=codes[:].bitcast(FP8X4), scales=scales[:], in_=bt_tiles[s][:].rearrange("p r t -> p (r t)")
            )
            bq_tiles[s] = (codes, scales)

        def score(s, j):
            g = (s % HEADS) // (HEADS // KEY_HEADS)
            codes, scales = bq_tiles[s]
            cols = slice(HALF * j, HALF * (j + 1))
            z = psum_z.tile([P, 512], F32, name="z")
            nc.tensor.matmul_mx(
                out=z[:],
                lhsT=codes[:].bitcast(FP8X4),
                lhsT_scale=scales[:],
                rhs=k_codes[g][:, cols].bitcast(FP8X4),
                rhs_scale=k_scales[g][:, cols],
                start=True,
                stop=True,
            )
            z_banks[s, j] = z

        def cap_tanh(s, j):
            if j == 0:
                tanh_tile = work.tile([P, KEYS], F32, name="tanh_tile")
                tanh_tiles[s] = tanh_tile
            nc.scalar.activation(
                out=tanh_tiles[s][:, HALF * j : HALF * (j + 1)],
                in_=z_banks[s, j][:],
                func=ACT.Tanh,
                scale=1.0 / (CAP * math.sqrt(FEATURES)),
            )

        def finish(s, j, who):
            m, h = divmod(s, HEADS)
            rows = slice(m * P, (m + 1) * P)
            if s not in results:
                result = work.tile([P, KEYS], F32, name="result")
                results[s] = result
            cols = slice(HALF * j, HALF * (j + 1))
            src, dst = tanh_tiles[s][:, cols], results[s][:, cols]
            if who == "g":
                dst, src = results[s][:], tanh_tiles[s][:]
                cap = work.tile([P, 1], F32, name="cap")
                nc.vector.memset(cap[:], CAP)
                nc.gpsimd.tensor_scalar(out=dst, in0=src, scalar1=cap[:], scalar2=0.0, op0=MULT, op1=ADD)
                nc.sync.dma_start(out=out[h, rows, :], in_=dst)
                return
            elif who == "s":
                nc.scalar.activation(out=dst, in_=src, func=ACT.Copy, scale=CAP)
            else:
                nc.vector.tensor_scalar(out=dst, in0=src, scalar1=CAP, scalar2=None, op0=MULT)
            nc.sync.dma_start(out=out[h, rows, cols], in_=dst)

        widen_x("vector", 0, 0)
        widen_x("scalar", 0, 2)
        widen_x("vector", 0, 1)
        widen_x("scalar", 0, 3)
        x_banks = [
            transpose_x(0, (0,), psum_z, "z"),
            transpose_x(0, (1,), psum_z, "z"),
            transpose_x(0, (2,), psum_y, "y"),
            transpose_x(0, (3,), psum_y, "y"),
        ]
        gain_banks = [psum_t.tile([P, 512], F32, name="tb"), psum_t.tile([P, 512], F32, name="tx")]
        for q in range(2):
            for e in range(2):
                nc.tensor.matmul(
                    out=gain_banks[q][:, e : 2 * PAIRS : 2],
                    lhsT=(minus_ones if q == 1 and e == 0 else ones)[:],
                    rhs=gain_row[:, q : 2 * PAIRS : 2],
                    start=True,
                    stop=True,
                )
        for g in range(2):
            widen_x("scalar", 1, g)
        for q in range(2):
            nc.scalar.copy(out=gains[:, q].rearrange("p i e -> p (i e)"), in_=gain_banks[q][:])
        for g in range(2, 4):
            widen_x("scalar", 1, g)
        scale_x(0, 0, x_banks[0])
        scale_x(0, 1, x_banks[1])
        quantize_x(0, 0, 1)
        scale_x(0, 2, x_banks[2])
        quantize_x(0, 1, 2)
        scale_x(0, 3, x_banks[3])
        quantize_x(0, 2, 3)
        x1_banks = [transpose_x(1, (0,), psum_t, "tx"), transpose_x(1, (1,), psum_y, "y")]
        quantize_x(0, 3, 4)
        project(0)
        make_table(0)
        square(0)
        project(1)
        square(1)
        scale_x(1, 0, x1_banks[0])
        scale_x(1, 1, x1_banks[1])
        mean_square((0,))
        inverse_root((0,))
        x1_banks += [transpose_x(1, (2,), psum_t, "tb"), transpose_x(1, (3,), psum_t, "tx")]
        k_banks = [transpose_keys(0, 0, psum_z, "z"), transpose_keys(0, 1, psum_z, "z")]
        group_keys(0, 0, k_banks[0])
        group_keys(0, 1, k_banks[1])
        scale_x(1, 2, x1_banks[2])
        scale_x(1, 3, x1_banks[3])
        mean_square((1,))
        inverse_root((1,))
        project(2)
        square(2)
        k_banks = [transpose_keys(0, 2, psum_z, "z"), transpose_keys(0, 3, psum_z, "z")]
        group_keys(0, 2, k_banks[0])
        group_keys(0, 3, k_banks[1])
        key_quants = {2: ((1, 0),), 3: ((1, 1),)}

        for s in range(UNITS):
            m, groups = X_STEPS.get(s, (0, ()))
            if s % 2 == 1 and s + 2 < UNITS:
                mean_square((s + 1, s + 2))
                inverse_root((s + 1, s + 2))
            if s >= 3 and finisher(s - 3, 0) == "g":
                finish(s - 3, 0, "g")
            next_m, next_groups = X_STEPS.get(s + 1, (0, ()))
            for g in next_groups:
                widen_x("scalar", next_m, g)
            if s + 3 < UNITS:
                project(s + 3)
                square(s + 3)
            if s >= 1:
                transpose_b(s - 1)
            if groups:
                x_bank = transpose_x(m, groups, psum_t, "tx")
            if s >= 1:
                group_b(s - 1)
            rotate_part(s, 0)
            rotate_part(s, 1)
            if s == 1:
                quantize_keys(0, 1)
            for i, g in enumerate(groups):
                scale_x(m, g, x_bank, i)
            if s == 0:
                quantize_x(1, 0, PASSES)
                quantize_keys(0, 0)
            if s >= 2:
                score(s - 2, 0)
                score(s - 2, 1)
                cap_tanh(s - 2, 0)
                cap_tanh(s - 2, 1)
            for j in range(2):
                if s >= 3 and finisher(s - 3, j) == "v":
                    finish(s - 3, j, "v")
            if s == UNITS - 1:
                quantize_b(s - 1)
            rotate_add(s)
            for g, j in key_quants.get(s, ()):
                quantize_keys(g, j)
            if s in TABLE_STEPS:
                make_table(TABLE_STEPS[s])
            for j in range(2):
                if s >= 3 and finisher(s - 3, j) == "s":
                    finish(s - 3, j, "s")
            if PASSES - 1 in groups:
                quantize_x(m, 0, PASSES)
            if 0 < s < UNITS - 1:
                quantize_b(s - 1)
            if s < 2:
                for i in (2 * s, 2 * s + 1):
                    group_keys(1, i, transpose_keys(1, i, psum_z, "z"))

        last = UNITS - 1
        finish(last - 2, 0, "g")
        score(last - 1, 0)
        score(last - 1, 1)
        transpose_b(last)
        cap_tanh(last - 1, 0)
        group_b(last)
        cap_tanh(last - 1, 1)
        quantize_b(last)
        finish(last - 1, 0, "v")
        score(last, 0)
        score(last, 1)
        cap_tanh(last, 0)
        finish(last - 1, 1, "v")
        cap_tanh(last, 1)
        finish(last, 0, "v")
        finish(last, 1, "v")
